import numpy as np, ml_dtypes
CORES = [16,18,20,22]
N = 4
BF = ml_dtypes.bfloat16
def gentries(a):
    return np.ascontiguousarray(a.reshape(8, 16, -1).transpose(0, 2, 1)).reshape(8, -1)
def gtable(e):
    e = np.asarray(e); return np.ascontiguousarray(e.reshape(8, -1, 16).transpose(0, 2, 1)).reshape(128, -1).astype(np.int32)
W, n, V, C, Z = 3, 4096, 8192, 2048, 1024
def counts(rng, h, z):
    c = np.zeros((N, 8, W), np.int64)
    for r in range(N):
        for g in range(8):
            m = int(h[r, g] - z[r, g]) - (W - 2); b = np.sort(rng.integers(0, m + 1, W - 3))
            c[r, g, 0] = n - h[r, g]; c[r, g, 1:W - 1] = np.diff(np.concatenate([[0], b, [m]])) + 1; c[r, g, W - 1] = z[r, g]
    return c
def some(rng):
    return rng.integers(C - C // 4, C + 1, (N, 8)), rng.integers(Z // 2, Z + 1, (N, 8))
def names(rng):
    return np.stack([np.stack([rng.permutation(V)[:n] for g in range(8)]) for r in range(N)]).astype(np.int64)
def depths(rng, c):
    return np.stack([np.stack([rng.permutation(np.repeat(np.arange(W), c[r, g])) for g in range(8)]) for r in range(N)])
def link(rng, o, dep):
    x = np.zeros((N, 8, n), np.int64)
    for r in range(N):
        q = (r + 1) % N
        for g in range(8):
            m = np.ones(V, bool); m[o[q, g]] = False; free = np.flatnonzero(m)
            v = free[rng.integers(0, len(free), n)]
            for k in range(1, W):
                i = np.flatnonzero(dep[r, g] == k)
                if len(i):
                    t = np.flatnonzero(dep[q, g] == k - 1 if k < W - 1 else dep[q, g] >= W - 2)
                    v[i] = o[q, g][t[rng.integers(0, len(t), len(i))]]
            x[r, g] = v
    return x
def pack(o, x, s):
    return {"own": np.stack([gtable(a) for a in o]), "nxt": np.stack([gtable(a) for a in x]), "pts": np.asarray(s).astype(np.int32)}
def points(rng):
    return rng.integers(0, 256, (N, 8, n))
def setup_inputs(rng):
    h, z = some(rng); o = names(rng); dep = depths(rng, counts(rng, h, z))
    return pack(o, link(rng, o, dep), points(rng))
def setup_inputs_full(rng):
    o = names(rng); c = counts(rng, np.full((N, 8), C), np.full((N, 8), Z)); e = rng.permutation(8)[:4]
    c[:, e, 1:W - 2] = 1; c[:, e, W - 2] = C - Z - (W - 3)
    dep = depths(rng, c)
    return pack(o, link(rng, o, dep), points(rng))
def setup_inputs_few(rng):
    h, z = some(rng); e = rng.permutation(8); q = int(rng.integers(0, N)); o = names(rng)
    z[:, e[2]] = 1; z[:, e[3]] = np.where(rng.random(N) < 0.5, 0, z[:, e[3]]); z[q, e[3]] = 0; z[:, e[4]] = Z; h[:, e[4]] = C
    c = counts(rng, h, z); c[:, e[0], 0] = n; c[:, e[0], 1:] = 0
    for t in range(W - 1):
        r = (q - t) % N; c[r, e[1], 0] += np.sum(c[r, e[1], t + 1:]); c[r, e[1], t + 1:] = 0
    dep = depths(rng, c)
    return pack(o, link(rng, o, dep), points(rng))
def setup_inputs_repeats(rng):
    h, z = some(rng); o = names(rng); dep = depths(rng, counts(rng, h, z)); x = link(rng, o, dep)
    for r in range(N):
        for g in range(8):
            for k in (0, W - 1):
                i = np.flatnonzero(dep[r, g] == k); x[r, g, i] = x[r, g, i[0]]
    return pack(o, x, points(rng))
def setup_inputs_ends(rng):
    h, z = some(rng); dep = depths(rng, counts(rng, h, z))
    o = 1 + np.stack([np.stack([rng.permutation(V - 2)[:n] for g in range(8)]) for r in range(N)]).astype(np.int64)
    for r in range(N):
        for g in range(0, 8, 2):
            o[r, g, 0] = 0; o[r, g, n - 1] = V - 1; a = dep[r, g]
            i = np.flatnonzero(a == W - 1); j = i[rng.integers(0, len(i))]; u, v = int(a[0]), int(a[j]); a[j] = u; a[0] = v
            i = np.flatnonzero(a[1:] == W - 1) + 1; j = i[rng.integers(0, len(i))]; u, v = int(a[n - 1]), int(a[j]); a[j] = u; a[n - 1] = v
    x = link(rng, o, dep)
    x[:, 0::2, 0] = V - 1; x[:, 0::2, n - 1] = 0
    for g in range(1, 8, 2):
        m = (dep[:, g] == 0) & (rng.random((N, n)) < 0.5)
        x[:, g] = np.where(m, rng.integers(0, 2, (N, n)) * (V - 1), x[:, g])
    return pack(o, x, 255 * rng.integers(0, 2, (N, 8, n)))
def setup_inputs_spread(rng):
    z = np.maximum(Z >> rng.integers(0, 7, (N, 8)), 1); h = z + np.maximum((C - Z) >> rng.integers(0, 7, (N, 8)), W - 2)
    o = np.stack([np.stack([(rng.integers(0, V) + rng.permutation(n + n // 8)[:n]) % V for g in range(8)]) for r in range(N)]).astype(np.int64)
    o[:, 1::2] = np.sort(o[:, 1::2], axis=2)
    dep = depths(rng, counts(rng, h, z))
    return pack(o, link(rng, o, dep), 255 >> rng.integers(0, 9, (N, 8, n)))
def followers(o, x):
    to = np.zeros((N, 8, n), np.int64)
    for r in range(N):
        for g in range(8):
            where = np.full(V, -1, np.int64); where[o[(r + 1) % N, g]] = np.arange(n); to[r, g] = where[x[r, g]]
    return to
def step(p, v, t):
    return np.take_along_axis(np.roll(v, -t, axis=0), p, axis=2)
def chains(to, s):
    p = np.broadcast_to(np.arange(n), (N, 8, n)); tot = s.astype(np.int64)
    for t in range(1, W):
        p = np.where(p >= 0, step(np.maximum(p, 0), to, t - 1), -1)
        tot = tot + np.where(p >= 0, step(np.maximum(p, 0), s, t), 0)
    return p, tot
def check_inputs(d):
    try:
        o = np.stack([gentries(a) for a in d["own"]]).astype(np.int64); x = np.stack([gentries(a) for a in d["nxt"]]).astype(np.int64); s = np.asarray(d["pts"]).astype(np.int64)
        if o.shape != (N, 8, n) or x.shape != (N, 8, n) or s.shape != (N, 8, n): return ["shapes"]
        bad = []
        if s.min() < 0 or s.max() > 255: bad.append("points")
        if o.min() < 0 or o.max() >= V or x.min() < 0 or x.max() >= V: return bad + ["names in range"]
        if (np.diff(np.sort(o, axis=2), axis=2) == 0).any(): return bad + ["own names differ"]
        to = followers(o, x); p, tot = chains(to, s)
        if np.max(np.count_nonzero(to >= 0, axis=2)) > C: bad.append("followers")
        if np.max(np.count_nonzero(p >= 0, axis=2)) > Z: bad.append("kept")
        return bad
    except Exception:
        return ["shapes"]
def reference(own, nxt, pts):
    o = np.stack([gentries(a) for a in own]).astype(np.int64); x = np.stack([gentries(a) for a in nxt]).astype(np.int64)
    p, tot = chains(followers(o, x), pts)
    yk = np.full((N, 8, Z), -1, np.float32); ys = np.zeros((N, 8, Z), np.float32)
    for r in range(N):
        for g in range(8):
            i = np.flatnonzero(p[r, g] >= 0)
            yk[r, g, :len(i)] = o[r, g, i]; ys[r, g, :len(i)] = tot[r, g, i]
    return {"yk": yk, "ys": ys}

@@ -1,0 +1,382 @@
+from concourse.mybir import AluOpType as A, ActivationFunctionType as F
+
+SCRATCH = {
+    "owi": ("sbuf", [128, 256], "int32"),
+    "pti": ("sbuf", [128, 256], "int32"),
+    "nxi": ("sbuf", [128, 256], "int32"),
+    "nls": ("sbuf", [128, 256], "uint16"),
+    "nl": ("sbuf", [128, 256], "uint16"),
+    "pb": ("sbuf", [128, 256], "bfloat16"),
+    "pfB": ("sbuf", [128, 128], "float32"),
+    "ltA": ("sbuf", [128, 128], "bfloat16"),
+    "htA": ("sbuf", [128, 128], "bfloat16"),
+    "ltB": ("sbuf", [128, 128], "float32"),
+    "htB": ("sbuf", [128, 128], "float32"),
+    "ol": ("sbuf", [128, 256], "uint16"),
+    "jl": ("sbuf", [128, 256], "uint16"),
+    "jy": ("sbuf", [128, 128], "uint16"),
+    "jx": ("sbuf", [128, 128], "uint16"),
+    "DA": ("sbuf", [128, 2048], "bfloat16"),
+    "DB": ("sbuf", [128, 2048], "float32"),
+    "WA": ("sbuf", [128, 8192], "bfloat16"),
+    "WB": ("sbuf", [128, 8192], "float32"),
+    "bg": ("sbuf", [128, 4096], "bfloat16"),
+    "R": ("sbuf", [128, 4112], "bfloat16"),
+    "V2": ("sbuf", [128, 4112], "bfloat16"),
+    "R2y": ("sbuf", [128, 2048], "bfloat16"),
+    "R2x": ("sbuf", [128, 2048], "bfloat16"),
+    "prow": ("sbuf", [8, 4096], "bfloat16"),
+    "pid": ("sbuf", [128, 1], "int32"),
+    "pm": ("sbuf", [128, 1], "int32"),
+    "hA": ("sbuf", [128, 1], "float32"),
+    "hB": ("sbuf", [128, 1], "float32"),
+    "ccol": ("sbuf", [128, 1], "float32"),
+    "padc": ("sbuf", [128, 1], "float32"),
+    "ci": ("sbuf", [128, 16], "float32"),
+    "cst": ("sbuf", [128, 16], "float32"),
+    "BZ": ("sbuf", [128, 704], "bfloat16"),
+    "BO": ("sbuf", [128, 400], "bfloat16"),
+    "NL": ("sbuf", [128, 128], "bfloat16"),
+    "E4": ("sbuf", [128, 144], "bfloat16"),
+    "ones": ("sbuf", [128, 256], "float32"),
+    "d3": ("sbuf", [128, 256], "bfloat16"),
+    "mi": ("sbuf", [128, 512], "float32"),
+    "mk": ("sbuf", [128, 2320], "bfloat16"),
+    "blk": ("sbuf", [128, 1024], "bfloat16"),
+    "bl": ("sbuf", [128, 64], "uint16"),
+    "blc": ("sbuf", [128, 64], "bfloat16"),
+    "off": ("sbuf", [128, 64], "uint16"),
+    "kYs": ("sbuf", [128, 128], "bfloat16"),
+    "kYl": ("sbuf", [128, 128], "bfloat16"),
+    "kX1": ("sbuf", [128, 128], "bfloat16"),
+    "kfs": ("sbuf", [128, 256], "bfloat16"),
+    "kfl": ("sbuf", [128, 256], "bfloat16"),
+    "kept": ("sbuf", [128, 256], "bfloat16"),
+    "zx": ("sbuf", [128, 32], "bfloat16"),
+    "e0": ("sbuf", [128, 16], "float32"),
+    "e1": ("sbuf", [128, 16], "float32"),
+    "p1": ("sbuf", [128, 16], "float32"),
+    "zl": ("sbuf", [128, 16], "uint16"),
+    "cum": ("sbuf", [128, 256], "float32"),
+    "KW": ("sbuf", [128, 256], "float32"),
+    "KV": ("sbuf", [128, 256], "float32"),
+    "YW": ("sbuf", [128, 256], "float32"),
+    "owf": ("sbuf", [128, 256], "float32"),
+    "hit": ("sbuf", [128, 1024], "bfloat16"),
+    "res": ("sbuf", [128, 1024], "float32"),
+}
+for _k in range(8):
+    SCRATCH["b%d" % _k] = ("psum", [128, 512], "float32")
+SEMAPHORES = ["v", "a", "t", "p", "down", "dptb", "dpts", "dnxt", "dda", "ddb", "dprow", "dwin", "dout",
+              "rn", "rv", "ry0", "ry1", "rx0", "rx1", "rk", "rf", "sent"]
+
+SUBS = [(0, 16), (16, 32)] + [(k, k + 32) for k in range(32, 224, 32)] + [(224, 240), (240, 256)]
+SENDS = [(0, 32), (32, 96), (96, 160), (160, 224), (224, 256)]
+NY = 128
+
+
+def rank_program(g, core, T, topo):
+    rank = T.rank_of(core)
+    if rank is None:
+        return
+    prv, nxc, opp = (T.cores[(rank + k) % 4] for k in (3, 1, 2))
+    queues = {"v": g.vector, "a": g.scalar, "t": g.tensor, "p": g, "s": g.sync}
+    cnt = {}
+    seen = {}
+
+    def need(q, toks):
+        best = {}
+        for s, n in toks:
+            best[s] = max(best.get(s, 0), n)
+        for s in sorted(best):
+            if seen.get((q, s), 0) < best[s]:
+                queues[q].wait_ge(T.sem[s], best[s])
+                seen[(q, s)] = best[s]
+
+    def done(s, ins, n):
+        cnt[s] = cnt.get(s, 0) + n
+        ins.then_inc(T.sem[s], n)
+        return (s, cnt[s])
+
+    def V(toks, name, *args):
+        need("v", toks)
+        q = g.vector
+        if name == "ts":
+            out, in0, s1, s2, op0 = args[:5]
+            ins = q.tensor_scalar(out, in0, s1, s2, op0, args[5]) if len(args) > 5 else q.tensor_scalar(out, in0, s1, s2, op0)
+        elif name == "tt":
+            ins = q.tensor_tensor(*args)
+        elif name == "cp":
+            ins = q.tensor_copy(*args)
+        elif name == "ms":
+            ins = q.memset(*args)
+        else:
+            ins = q.tensor_tensor_scan(*args)
+        return done("v", ins, 1)
+
+    def ACT(toks, out, in_, func, bias=None, scale=None):
+        need("a", toks)
+        if scale is not None:
+            ins = g.scalar.activation(out, in_, func, scale=scale)
+        elif bias is not None:
+            ins = g.scalar.activation(out, in_, func, bias=bias)
+        else:
+            ins = g.scalar.activation(out, in_, func)
+        return done("a", ins, 1)
+
+    def IOTA(toks, out, pattern, base, cm, small=True):
+        need("p", toks)
+        ins = g.iota(out, pattern, base, cm, allow_small_or_imprecise_dtypes=True) if small else g.iota(out, pattern, base, cm)
+        return done("p", ins, 1)
+
+    def SEL(toks, buf, pattern, cmp, fill, base, cm):
+        need("p", toks)
+        return done("p", g.affine_select(buf, buf, pattern, cmp, fill, base, cm), 1)
+
+    def SELO(toks, out, src, pattern, cmp, base, cm):
+        need("p", toks)
+        return done("p", g.affine_select(out, src, pattern, cmp, 0.0, base, cm), 1)
+
+    def DMA(q, s, toks, out, in_):
+        need(q, toks)
+        return done(s, queues[q].dma_start(out, in_), 16)
+
+    def MM(toks, jobs, tok=True):
+        need("t", toks)
+        ins = None
+        for out, lhs, rhs, st, sp in jobs:
+            ins = g.tensor.matmul(out, lhs, rhs, st, sp)
+        return done("t", ins, 1) if tok else None
+
+    def SEND(toks, to, dst, src, sem):
+        need("p", toks)
+        rid, pid, _se = topo.addr(to)
+        g.remote_dma(out_ap=dst, in_ap=src, remote_sem=T.sem[sem], local_sem=T.sem.sent, pid=pid, routing_id=rid,
+                     dma_engine_mask=topo.mask(core, to))
+        n = len(topo.engines(core, to))
+        cnt["sent"] = cnt.get("sent", 0) + n
+        cnt[sem] = cnt.get(sem, 0) + n
+        return (sem, cnt[sem])
+
+    def moved(mat, t, K=128):
+        buf, c = mat
+        return buf[0:K, c + 15 - t:c + 143 - t]
+
+    def rewrap(out, mat, src, c0, c1, K=128, close=True, first=True):
+        return [(out, moved(mat, t, K), src[0:K, 16 * c0 + t:16 * c1:16], first and t == 0, close and t == 15)
+                for t in range(16)]
+
+    def el(buf, c0, c1):
+        return buf[:, 16 * c0:16 * c1]
+
+    l_own = DMA("s", "down", [], T.owi[:], T.own[:])
+    l_ptb = DMA("a", "dptb", [], T.pti[:, 128:256], T.pts[:, 2048:4096])
+    l_pts = DMA("a", "dpts", [], T.pti[:, 0:128], T.pts[:, 0:2048])
+    l_nxt = DMA("s", "dnxt", [], T.nxi[:], T.nxt[:])
+
+    c_pid = IOTA([], T.pid[:], [[1, 1]], 0, 1, False)
+    c_lta = IOTA([], T.ltA[:], [[-16, 128]], 2048, 0)
+    c_ltb = IOTA([], T.ltB[:], [[-16, 128]], 2048, 0)
+    z0 = V([], "ms", T.WB[:, 0:128], 0.0)
+    v_da = V([], "ms", T.DA[:], 0.0)
+    z1 = V([], "ms", T.WB[:, 256:1024], 0.0)
+    v_db = V([], "ms", T.DB[:, 0:640], 0.0)
+    v_pm = V([c_pid], "ts", T.pm[:], T.pid[:], 15, None, A.bitwise_and)
+    v_ha = V([v_pm], "ts", T.hA[:], T.pm[:], -16.0, 496.0, A.mult, A.add)
+    v_hb = V([v_pm], "ts", T.hB[:], T.pm[:], -16.0, 240.0, A.mult, A.add)
+    a1 = ACT([z0], T.WB[:, 128:256], T.WB[:, 0:128], F.Silu)
+    ACT([a1, z1], T.DB[:, 640:1664], T.WB[:, 0:1024], F.Silu)
+    a2 = ACT([], T.DB[:, 1664:2048], T.WB[:, 0:384], F.Silu)
+    a_htb = ACT([v_hb], T.htB[:], T.WB[:, 0:128], F.Identity, T.hB[:])
+    a_hta = ACT([v_ha], T.htA[:], T.WB[:, 0:128], F.Identity, T.hA[:])
+    a3 = ACT([], T.WB[:, 1024:2048], T.WB[:, 0:1024], F.Silu)
+    ACT([a3], T.WB[:, 2048:4096], T.WB[:, 0:2048], F.Silu)
+    a5 = ACT([a3], T.WB[:, 4096:5248], T.WB[:, 0:1152], F.Silu)
+    v_pfb = V([l_ptb], "ts", T.pfB[:], T.pti[:, 128:256], 16.0, 16.0, A.mult, A.add)
+    V([], "ms", T.WA[:, 0:2048], 0.0)
+    v_ol = V([l_own], "cp", T.ol[:], T.owi[:])
+    v_pb = V([l_pts], "ts", T.pb[:], T.pti[:], 16.0, 16.0, A.mult, A.add)
+    V([], "ms", T.WA[:, 2048:5120], 0.0)
+    v_nls = V([l_nxt], "cp", T.nls[:], T.nxi[:])
+    v_wa = V([], "ms", T.WA[:, 5120:8192], 0.0)
+    DMA("s", "dda", [v_da, c_lta], T.DA[1::16, :], T.ltA[:])
+    DMA("s", "ddb", [v_db, a2, c_ltb], T.DB[1::16, :], T.ltB[:])
+    DMA("s", "ddb", [v_pfb], T.DB[2::16, :], T.pfB[:])
+    d_b = DMA("s", "ddb", [a_htb], T.DB[0::16, :], T.htB[:])
+    DMA("s", "dda", [a_hta], T.DA[0::16, :], T.htA[:])
+    d_a = DMA("s", "dda", [v_pb], T.DA[2::16, :], T.pb[:, 0:128])
+    DMA("s", "dprow", [], T.prow[:, 0:2048], T.pb[:, 0:128])
+    d_prow = DMA("s", "dprow", [], T.prow[:, 2048:4096], T.pb[:, 128:256])
+
+    IOTA([], T.WB[:, 5248:6720], [[0, 1472]], 0, 0)
+    p_z2 = IOTA([], T.WB[:, 6720:8192], [[0, 1472]], 0, 0)
+    r_n = SEND([v_nls], nxc, T.nl[:], T.nls[:], "rn")
+    p_z = IOTA([], T.BZ[:], [[0, 704]], 0, 0)
+
+    s_b = ACT([a5, p_z2, v_ol, d_b], T.WB[:].indirect(T.ol[:, 128:256]), T.DB[:], F.Silu)
+    s_a = V([v_wa, v_ol, d_a], "cp", T.WA[:].indirect(T.ol[:, 0:128]), T.DA[:])
+
+    BI, B2, B0, B8 = ((T.BZ, 144 * k) for k in range(4))
+    ID = T.BZ[:, 576:704]
+    E = (T.BO, 0)
+    E256 = (T.E4, 0)
+    LS = T.BO[:, 144:272]
+    SG = T.BO[:, 272:400]
+
+    def rowsel(mat, fills):
+        buf = mat[0][:, mat[1]:mat[1] + 144]
+        tok = p_z
+        for k, w in fills:
+            tok = SEL([tok], buf, [[-16, 9], [0, 16]], A.not_equal, w, -k, 1)
+        return SEL([tok], buf, [[0, 9], [1, 16]], A.is_equal, 0.0, -15, 0)
+
+    m_bi = rowsel(BI, [(0, 8.0), (1, 0.0625)])
+    m_b8 = SEL([p_z], T.BZ[:, 432:576], [[-1, 144]], A.not_equal, 0.0625, 15, 16)
+    m_b2 = rowsel(B2, [(2, 0.0625)])
+    IOTA([], T.R[:, 4096:4112], [[0, 16]], 0, 0)
+    IOTA([], T.V2[:, 4096:4112], [[0, 16]], 0, 0)
+    v_zx = IOTA([], T.zx[:], [[0, 32]], 0, 0)
+    m_id = SEL([p_z], ID, [[-1, 128]], A.not_equal, 1.0, 0, 1)
+    IOTA([], T.BO[:, 128:144], [[0, 16]], 0, 0)
+    p_one = IOTA([], SG, [[0, 128]], 1, 0)
+
+    MM([m_b8, d_prow], rewrap(T.b7[:, 0:128], B8, T.prow, 0, 128, 8, False)
+       + rewrap(T.b5[:, 0:128], B8, T.prow, 128, 256, 8, False), False)
+
+    def tlist(out, src, c0, c1):
+        return [(out[0:c1 - c0, t:128:16], src[:, 16 * c0 + t:16 * c1:16], T.BZ[:, 159:287:16], True, True)
+                for t in range(16)]
+
+    g_a = [ACT([s_b, r_n], el(T.bg, c0, c1), T.WB[:].indirect(T.nl[:, c0:c1]), F.Copy) for c0, c1 in SUBS]
+    upto = {}
+    t_code = [None] * 4
+    v_jl = [None] * 4
+
+    def jl(q):
+        v_jl[q] = V([t_code[q]], "ts", T.jl[:, 64 * q:64 * q + 64], T["b%d" % q][:, 0:64], -1.0, 4096.0, A.mult, A.add)
+
+    r_y, r_x = [], []
+    for k, (c0, c1) in enumerate(SUBS):
+        upto[c1] = V([s_a, g_a[k], r_n], "tt", el(T.R, c0, c1), T.WA[:].indirect(T.nl[:, c0:c1]), el(T.bg, c0, c1), A.add)
+        for s0, s1 in SENDS:
+            if s1 == c1:
+                r_v = SEND([upto[c1]], opp, el(T.V2, s0, s1), el(T.R, s0, s1), "rv")
+        if c1 % 64 == 0:
+            q = c1 // 64 - 1
+            t_code[q] = MM([upto[c1], m_bi], rewrap(T["b%d" % q][:, 0:64], BI, T.R, 64 * q, 64 * q + 64))
+            if q == 1:
+                MM([m_b2], tlist(T.b6[:, 0:128], T.R, 0, 128), False)
+        if c1 == 32:
+            m = SEL([p_one], SG, [[-16, 8], [0, 16]], A.is_ge, 0.0, 0, 1)
+        if c1 == 96:
+            m_sg = SEL([m], SG, [[16, 8], [0, 16]], A.is_ge, 0.0, 15, -1)
+        if c1 == 128:
+            jl(0)
+            r_y.append(SEND([v_jl[0]], nxc, T.jy[:, 0:64], T.jl[:, 0:64], "ry0"))
+        if c1 == 160:
+            m_e = SELO([m_sg], T.BO[:, 0:128], SG, [[0, 8], [1, 16]], A.is_equal, -15, 0)
+        if c1 == 192:
+            jl(1)
+            r_y.append(SEND([v_jl[1]], nxc, T.jy[:, 64:NY], T.jl[:, 64:NY], "ry1"))
+        if c1 == 240:
+            jl(2)
+            r_x.append(SEND([v_jl[2]], prv, T.jx[:, 0:192 - NY], T.jl[:, NY:192], "rx0"))
+
+    gy2 = []
+    for r, (c0, cm, c1) in zip(r_y, ((0, 32, 64), (64, 96, NY))):
+        gy2.append(V([upto[256], r, v_zx], "cp", el(T.R2y, c0, cm), T.R[:].indirect(T.jy[:, c0:cm])))
+        gy2.append(ACT([upto[256], r, v_zx], el(T.R2y, cm, c1), T.R[:].indirect(T.jy[:, cm:c1]), F.Copy))
+        if c0 == 0:
+            v_owf = V([l_own], "cp", T.owf[:], T.owi[:])
+            jl(3)
+            r_x.append(SEND([v_jl[3]], prv, T.jx[:, 192 - NY:256 - NY], T.jl[:, 192:256], "rx1"))
+    c_ci = IOTA([], T.ci[:], [[1, 16]], 1025, 0)
+    t_kf = MM([m_b2], tlist(T.b6[:, 128:256], T.R, 128, 256))
+    a_kf = ACT([t_kf], T.kfs[:], T.b6[:, 0:256], F.Copy)
+    r_f = SEND([a_kf], prv, T.kfl[:], T.kfs[:], "rf")
+    t_ky = MM(gy2 + [v_jl[0]], tlist(T.b0, T.R2y, 0, NY))
+    a_ky = ACT([t_ky], T.kYs[:], T.b0[:, 0:128], F.Copy)
+    r_k = SEND([a_ky], opp, T.kYl[:], T.kYs[:], "rk")
+    p_ones = IOTA([], T.ones[:], [[0, 256]], 1, 0)
+    c_d3 = IOTA([], T.d3[:], [[16, 16], [256, 16]], 0, 0)
+    m_ls = SELO([m_sg], LS, SG, [[1, 128]], A.is_gt, 0, -1)
+    m_nl = SELO([m_sg], T.NL[:], SG, [[-1, 128]], A.is_gt, 0, 1)
+    m_b0 = rowsel(B0, [(0, 0.0625)])
+    c_mi = IOTA([], T.mi[:], [[1, 512]], 0, 0)
+
+    def gx(c0, c1):
+        return el(T.R2x, c0 - NY, c1 - NY), T.V2[:].indirect(T.jx[:, c0 - NY:c1 - NY])
+
+    g1 = [V([r_v, r_x[0], v_zx], "cp", *gx(128, 164)), ACT([r_v, r_x[0], v_zx], *gx(164, 192), F.Copy)]
+    g2 = [V([r_x[1]], "cp", *gx(192, 224)), ACT([r_x[1]], *gx(224, 256), F.Copy)]
+    DMA("s", "dwin", [v_owf, g_a[-1], g2[1]], T.WB[0::16, 0:4096], T.owf[:])
+
+    def back(bank, c0, c1, kt):
+        n = c1 - c0
+        return [(bank[:, 0:n], kt[0:n, :], ID[0:n, 0:n], True, True)]
+
+    def plus(bank, kt, last):
+        return [(bank[:, 0:128], kt, ID, False, last)]
+
+    def kept(bank, c0, c1, tok):
+        return V([tok], "ts", T.kept[:, c0:c1], bank[:, 0:c1 - c0], 0.5, None, A.is_gt)
+
+    def zsum(s0, s1, first, last):
+        return [(T.b4[:, 0:16], moved(E, s), T.kept[:, 16 * s:16 * s + 16], first and s == s0, last and s == s1 - 1)
+                for s in range(s0, s1)]
+
+    MM([r_f, m_id], plus(T.b7, T.kfl[:, 0:128], False) + plus(T.b5, T.kfl[:, 128:256], False), False)
+    t_k1 = MM(g1 + g2 + [v_jl[1]], tlist(T.b1, T.R2x, 0, 128))
+    v_padc = V([], "ts", T.padc[:], T.pm[:], 0.5, -1.0, A.is_lt, A.mult)
+    v_cc = V([], "ts", T.ccol[:], T.pm[:], 16.0, None, A.mult)
+    v_cst = V([v_cc, c_ci], "ts", T.cst[:], T.ci[:], T.ccol[:], None, A.add)
+    t_by = MM([r_k, v_jl[3], m_id], back(T.b3, 0, NY, T.kYl))
+    t_y0 = MM([], plus(T.b7, T.kYl[:], True))
+    a_k1 = ACT([t_k1], T.kX1[:], T.b1[:, 0:128], F.Copy)
+    c_mk = ACT([], T.mk[:, 0:1024], T.V2[:, 0:1024], F.Copy, None, 0.0)
+    v_cy = kept(T.b3, 0, NY, t_by)
+    t_b1 = MM([a_k1], back(T.b0, 128, 256, T.kX1))
+    MM([v_cy, m_e], zsum(0, 8, True, False), False)
+    v_c1 = kept(T.b0, 128, 256, t_b1)
+    v_e4 = V([m_e], "ts", T.E4[:], T.BO[:, 0:144], 256.0, None, A.mult)
+    t_z = MM([v_c1, v_jl[2]], zsum(8, 16, False, True))
+    v_zc = V([t_z, v_zx, v_cst, p_ones], "scan", T.zx[:, 1:17], T.ones[:, 0:16], T.b4[:, 0:16], 0.0, A.mult, A.add)
+    t_y1 = MM([], plus(T.b5, T.kX1[:], True))
+    ACT([t_y0], T.YW[:, 0:128], T.b7[:, 0:128], F.Identity, -3.0)
+    a_yw = ACT([t_y1], T.YW[:, 128:256], T.b5[:, 0:128], F.Identity, -3.0)
+    DMA("s", "dwin", [a_yw], T.WB[1::16, 0:4096], T.YW[:])
+    t_off = MM([v_zc, m_ls], [(T.b1[:, 128:129], LS, T.zx[:, 16:17], True, True)])
+    v_e0 = V([t_z], "ts", T.e0[:], T.b4[:, 0:16], 0.0, None, A.is_equal)
+    v_e1 = V([v_e0, v_cst], "tt", T.e1[:], T.e0[:], T.cst[:], A.mult)
+    v_p1 = V([v_e1, v_zc], "tt", T.p1[:], T.e1[:], T.zx[:, 0:16], A.add)
+    v_zl = V([v_p1, t_off], "ts", T.zl[:], T.p1[:], T.b1[:, 128:129], None, A.add)
+    MM([m_sg], [(T.b3[:, 0:256], SG, T.kept[:], True, True)], False)
+    t_n1 = MM([m_nl], [(T.b3[:, 256:512], T.NL[:], T.kept[:], True, True)])
+    v_pad = ACT([v_padc, c_mk], T.WB[:, 4096:4352], T.mk[:, 0:256], F.Identity, T.padc[:])
+    v_mks = V([v_zl, c_mk, v_pad, c_d3], "cp", T.mk[:].indirect(T.zl[:]), T.d3[:])
+    v_b0 = V([v_mks], "scan", T.blk[:, 0:512], T.mk[:, 0:512], T.mk[:, 0:512], 0.0, A.max, A.max)
+    v_b1 = V([v_b0], "scan", T.blk[:, 512:1024], T.mk[:, 512:1024], T.mk[:, 512:1024], T.blk[:, 511:512], A.max, A.max)
+    t_bl = [MM([v_b, m_b0], rewrap(b[:, 0:32], B0, T.blk, 32 * h, 32 * h + 32))
+            for h, (v_b, b) in enumerate(((v_b0, T.b0), (v_b1, T.b1)))]
+    v_cum = V([t_n1], "scan", T.cum[:], T.ones[:], T.b3[:, 0:256], 0.0, A.mult, A.add)
+    v_kw = V([v_cum], "tt", T.KW[:], T.cum[:], T.b3[:, 256:512], A.subtract)
+    a_kv = ACT([v_kw], T.KV[:], T.KW[:], F.Identity, -512.0)
+    v_bl, v_hit = [], []
+    for h, (b, kw, tok) in enumerate(((T.b0, T.KW, v_kw), (T.b1, T.KV, a_kv))):
+        lst = T.bl[:, 32 * h:32 * h + 32]
+        v_bl.append(V([t_bl[h]], "cp", lst, b[:, 0:32]))
+        v_hit.append(V([tok, v_bl[h], c_mi], "tt", T.hit[:, 512 * h:512 * h + 512], kw[:].indirect(lst), T.mi[:], A.is_le))
+    t_h = []
+    for h, (b, o) in enumerate(((T.b0, T.b2), (T.b1, T.b6))):
+        a_bc = ACT([v_bl[h]], T.blc[:, 32 * h:32 * h + 32], b[:, 0:32], F.Copy)
+        MM([a_bc], [(o[:, 0:32], ID, T.blc[:, 32 * h:32 * h + 32], True, False)], False)
+        t_h.append(MM([v_hit[h], v_e4], rewrap(o[:, 0:32], E256, T.hit, 32 * h, 32 * h + 32, first=False)))
+    v_of = [V([t_h[h]], "cp", T.off[:, 32 * h:32 * h + 32], o[:, 0:32]) for h, o in enumerate((T.b2, T.b6))]
+    win = T.WB[:, 0:4352]
+    rows = [v_pad, ("dwin", cnt["dwin"])]
+    ACT([v_of[0]] + rows, T.res[:, 0:512], win.indirect(T.off[:, 0:32]), F.Copy)
+    v_r = V([v_of[1]] + rows, "cp", T.res[:, 512:768], win.indirect(T.off[:, 32:48]))
+    a_r = ACT([v_of[1]], T.res[:, 768:1024], win.indirect(T.off[:, 48:64]), F.Copy)
+    DMA("s", "dout", [a_r, v_r], T.yk[:], T.res[0::16, :])
+    DMA("a", "dout", [a_r, v_r], T.ys[:], T.res[1::16, :])
+    need("p", [(s, cnt[s]) for s in sorted(cnt)])

@@ -4,75 +4,66 @@ SCRATCH = {
     "owi": ("sbuf", [128, 256], "int32"),
     "pti": ("sbuf", [128, 256], "int32"),
     "nxi": ("sbuf", [128, 256], "int32"),
+    "ols": ("sbuf", [128, 256], "uint16"),
+    "ol": ("sbuf", [128, 256], "uint16"),
+    "pfs": ("sbuf", [128, 256], "float32"),
+    "pf": ("sbuf", [128, 256], "float32"),
     "nls": ("sbuf", [128, 256], "uint16"),
     "nl": ("sbuf", [128, 256], "uint16"),
     "pb": ("sbuf", [128, 256], "bfloat16"),
-    "pfB": ("sbuf", [128, 128], "float32"),
-    "ltA": ("sbuf", [128, 128], "bfloat16"),
-    "htA": ("sbuf", [128, 128], "bfloat16"),
-    "ltB": ("sbuf", [128, 128], "float32"),
-    "htB": ("sbuf", [128, 128], "float32"),
-    "ol": ("sbuf", [128, 256], "uint16"),
     "jl": ("sbuf", [128, 256], "uint16"),
-    "jy": ("sbuf", [128, 128], "uint16"),
-    "jx": ("sbuf", [128, 128], "uint16"),
-    "DA": ("sbuf", [128, 2048], "bfloat16"),
-    "DB": ("sbuf", [128, 2048], "float32"),
+    "jx": ("sbuf", [128, 256], "uint16"),
+    "D": ("sbuf", [128, 2048], "float32"),
     "WA": ("sbuf", [128, 8192], "bfloat16"),
     "WB": ("sbuf", [128, 8192], "float32"),
     "bg": ("sbuf", [128, 4096], "bfloat16"),
     "R": ("sbuf", [128, 4112], "bfloat16"),
-    "V2": ("sbuf", [128, 4112], "bfloat16"),
-    "R2y": ("sbuf", [128, 2048], "bfloat16"),
-    "R2x": ("sbuf", [128, 2048], "bfloat16"),
+    "R2": ("sbuf", [128, 4096], "bfloat16"),
     "prow": ("sbuf", [8, 4096], "bfloat16"),
     "pid": ("sbuf", [128, 1], "int32"),
-    "pm": ("sbuf", [128, 1], "int32"),
-    "hA": ("sbuf", [128, 1], "float32"),
-    "hB": ("sbuf", [128, 1], "float32"),
-    "ccol": ("sbuf", [128, 1], "float32"),
-    "padc": ("sbuf", [128, 1], "float32"),
-    "ci": ("sbuf", [128, 16], "float32"),
-    "cst": ("sbuf", [128, 16], "float32"),
-    "BZ": ("sbuf", [128, 704], "bfloat16"),
+    "h8": ("sbuf", [128, 1], "int32"),
+    "o1": ("sbuf", [128, 1], "int32"),
+    "s16": ("sbuf", [128, 1], "float32"),
+    "sc": ("sbuf", [128, 1], "float32"),
+    "ev": ("sbuf", [128, 1], "float32"),
+    "jj": ("sbuf", [128, 8], "float32"),
+    "hb": ("sbuf", [128, 8], "float32"),
+    "xx": ("sbuf", [128, 256], "float32"),
+    "pr": ("sbuf", [8, 288], "int32"),
+    "pri": ("sbuf", [128, 18], "int32"),
+    "K": ("sbuf", [128, 4], "float32"),
+    "K2": ("sbuf", [128, 4], "float32"),
+    "swp": ("sbuf", [128, 18], "uint16"),
+    "BZ": ("sbuf", [128, 424], "bfloat16"),
     "BO": ("sbuf", [128, 400], "bfloat16"),
-    "NL": ("sbuf", [128, 128], "bfloat16"),
-    "E4": ("sbuf", [128, 144], "bfloat16"),
-    "ones": ("sbuf", [128, 256], "float32"),
-    "d3": ("sbuf", [128, 256], "bfloat16"),
-    "mi": ("sbuf", [128, 512], "float32"),
-    "mk": ("sbuf", [128, 2320], "bfloat16"),
-    "blk": ("sbuf", [128, 1024], "bfloat16"),
-    "bl": ("sbuf", [128, 64], "uint16"),
-    "blc": ("sbuf", [128, 64], "bfloat16"),
+    "cv": ("sbuf", [128, 272], "bfloat16"),
+    "d0": ("sbuf", [128, 512], "bfloat16"),
+    "mk": ("sbuf", [128, 4240], "bfloat16"),
+    "S": ("sbuf", [128, 1024], "bfloat16"),
+    "hit": ("sbuf", [128, 1024], "bfloat16"),
     "off": ("sbuf", [128, 64], "uint16"),
-    "kYs": ("sbuf", [128, 128], "bfloat16"),
-    "kYl": ("sbuf", [128, 128], "bfloat16"),
-    "kX1": ("sbuf", [128, 128], "bfloat16"),
+    "kX": ("sbuf", [128, 256], "bfloat16"),
     "kfs": ("sbuf", [128, 256], "bfloat16"),
     "kfl": ("sbuf", [128, 256], "bfloat16"),
     "kept": ("sbuf", [128, 256], "bfloat16"),
+    "loc": ("sbuf", [128, 272], "bfloat16"),
+    "DT": ("sbuf", [128, 272], "bfloat16"),
     "zx": ("sbuf", [128, 32], "bfloat16"),
     "e0": ("sbuf", [128, 16], "float32"),
-    "e1": ("sbuf", [128, 16], "float32"),
-    "p1": ("sbuf", [128, 16], "float32"),
-    "zl": ("sbuf", [128, 16], "uint16"),
-    "cum": ("sbuf", [128, 256], "float32"),
-    "KW": ("sbuf", [128, 256], "float32"),
-    "KV": ("sbuf", [128, 256], "float32"),
+    "e1": ("sbuf", [128, 17], "float32"),
+    "p1": ("sbuf", [128, 17], "float32"),
+    "zl": ("sbuf", [128, 18], "uint16"),
     "YW": ("sbuf", [128, 256], "float32"),
     "owf": ("sbuf", [128, 256], "float32"),
-    "hit": ("sbuf", [128, 1024], "bfloat16"),
     "res": ("sbuf", [128, 1024], "float32"),
 }
 for _k in range(8):
     SCRATCH["b%d" % _k] = ("psum", [128, 512], "float32")
-SEMAPHORES = ["v", "a", "t", "p", "down", "dptb", "dpts", "dnxt", "dda", "ddb", "dprow", "dwin", "dout",
-              "rn", "rv", "ry0", "ry1", "rx0", "rx1", "rk", "rf", "sent"]
+SEMAPHORES = ["v", "a", "t", "p", "down", "dpts", "dnxt", "dd", "dprow", "dk", "dwin", "dout",
+              "rp", "ro", "rn", "rx0", "rx1", "rx2", "rx3", "rf", "sent"]
 
 SUBS = [(0, 16), (16, 32)] + [(k, k + 32) for k in range(32, 224, 32)] + [(224, 240), (240, 256)]
-SENDS = [(0, 32), (32, 96), (96, 160), (160, 224), (224, 256)]
-NY = 128
+XV, XA, XP1 = 2176, 6272, 512
 
 
 def rank_program(g, core, T, topo):
@@ -116,7 +107,9 @@ def rank_program(g, core, T, topo):
 
     def ACT(toks, out, in_, func, bias=None, scale=None):
         need("a", toks)
-        if scale is not None:
+        if scale is not None and bias is not None:
+            ins = g.scalar.activation(out, in_, func, bias=bias, scale=scale)
+        elif scale is not None:
             ins = g.scalar.activation(out, in_, func, scale=scale)
         elif bias is not None:
             ins = g.scalar.activation(out, in_, func, bias=bias)
@@ -148,12 +141,13 @@ def rank_program(g, core, T, topo):
             ins = g.tensor.matmul(out, lhs, rhs, st, sp)
         return done("t", ins, 1) if tok else None
 
-    def SEND(toks, to, dst, src, sem):
+    def SEND(toks, to, dst, src, sem, step=1):
         need("p", toks)
         rid, pid, _se = topo.addr(to)
+        engines = topo.engines(core, to)[::step]
         g.remote_dma(out_ap=dst, in_ap=src, remote_sem=T.sem[sem], local_sem=T.sem.sent, pid=pid, routing_id=rid,
-                     dma_engine_mask=topo.mask(core, to))
-        n = len(topo.engines(core, to))
+                     dma_engine_mask=sum(1 << e for e in engines))
+        n = len(engines)
         cnt["sent"] = cnt.get("sent", 0) + n
         cnt[sem] = cnt.get(sem, 0) + n
         return (sem, cnt[sem])
@@ -169,214 +163,192 @@ def rank_program(g, core, T, topo):
     def el(buf, c0, c1):
         return buf[:, 16 * c0:16 * c1]
 
+    l_pts = DMA("s", "dpts", [], T.pti[:], T.pts[:])
     l_own = DMA("s", "down", [], T.owi[:], T.own[:])
-    l_ptb = DMA("a", "dptb", [], T.pti[:, 128:256], T.pts[:, 2048:4096])
-    l_pts = DMA("a", "dpts", [], T.pti[:, 0:128], T.pts[:, 0:2048])
     l_nxt = DMA("s", "dnxt", [], T.nxi[:], T.nxt[:])
 
     c_pid = IOTA([], T.pid[:], [[1, 1]], 0, 1, False)
-    c_lta = IOTA([], T.ltA[:], [[-16, 128]], 2048, 0)
-    c_ltb = IOTA([], T.ltB[:], [[-16, 128]], 2048, 0)
-    z0 = V([], "ms", T.WB[:, 0:128], 0.0)
-    v_da = V([], "ms", T.DA[:], 0.0)
-    z1 = V([], "ms", T.WB[:, 256:1024], 0.0)
-    v_db = V([], "ms", T.DB[:, 0:640], 0.0)
-    v_pm = V([c_pid], "ts", T.pm[:], T.pid[:], 15, None, A.bitwise_and)
-    v_ha = V([v_pm], "ts", T.hA[:], T.pm[:], -16.0, 496.0, A.mult, A.add)
-    v_hb = V([v_pm], "ts", T.hB[:], T.pm[:], -16.0, 240.0, A.mult, A.add)
-    a1 = ACT([z0], T.WB[:, 128:256], T.WB[:, 0:128], F.Silu)
-    ACT([a1, z1], T.DB[:, 640:1664], T.WB[:, 0:1024], F.Silu)
-    a2 = ACT([], T.DB[:, 1664:2048], T.WB[:, 0:384], F.Silu)
-    a_htb = ACT([v_hb], T.htB[:], T.WB[:, 0:128], F.Identity, T.hB[:])
-    a_hta = ACT([v_ha], T.htA[:], T.WB[:, 0:128], F.Identity, T.hA[:])
-    a3 = ACT([], T.WB[:, 1024:2048], T.WB[:, 0:1024], F.Silu)
-    ACT([a3], T.WB[:, 2048:4096], T.WB[:, 0:2048], F.Silu)
-    a5 = ACT([a3], T.WB[:, 4096:5248], T.WB[:, 0:1152], F.Silu)
-    v_pfb = V([l_ptb], "ts", T.pfB[:], T.pti[:, 128:256], 16.0, 16.0, A.mult, A.add)
-    V([], "ms", T.WA[:, 0:2048], 0.0)
-    v_ol = V([l_own], "cp", T.ol[:], T.owi[:])
-    v_pb = V([l_pts], "ts", T.pb[:], T.pti[:], 16.0, 16.0, A.mult, A.add)
+    c_j = IOTA([], T.jj[:], [[-4, 8]], 48, 0)
+    c_x = IOTA([], T.xx[:], [[1, 256]], 0, 0)
+    z0 = V([], "ms", T.WB[:, 0:64], 0.0)
+    v_h8 = V([c_pid], "ts", T.h8[:], T.pid[:], 8, None, A.bitwise_and)
+    v_o1 = V([], "ts", T.o1[:], T.pid[:], 1, None, A.bitwise_and)
+    v_s = V([v_h8], "ts", T.s16[:], T.h8[:], 4.0, -16.0, A.mult, A.add)
+    V([], "ms", T.WA[:, 0:256], 0.0)
+    v_sc = V([v_s, v_o1], "ts", T.sc[:], T.o1[:], T.s16[:], None, A.mult)
+    V([], "ms", T.WA[:, 256:512], 0.0)
+    v_ev = V([v_sc], "ts", T.ev[:], T.s16[:], T.sc[:], None, A.subtract)
+    V([], "ms", T.WA[:, 512:768], 0.0)
+    v_bias = V([v_ev, c_j], "ts", T.hb[:], T.jj[:], T.s16[:], T.ev[:], A.subtract, A.mult)
+    V([], "ms", T.WA[:, 768:1536], 0.0)
+    v_pf = V([l_pts], "ts", T.pfs[:], T.pti[:], 1.0, T.s16[:], A.add, A.mult)
+    V([], "ms", T.WA[:, 1536:2048], 0.0)
+    v_ols = V([l_own], "cp", T.ols[:], T.owi[:])
+    z1 = V([], "ms", T.WB[:, 128:XV], 0.0)
+    a1 = ACT([z0], T.WB[:, 64:128], T.WB[:, 0:64], F.Silu)
+    for j in range(8):
+        a_d = ACT([v_bias, c_x], T.D[:, 256 * j:256 * j + 256], T.xx[:], F.Identity, T.hb[:, j:j + 1], T.sc[:])
+    ACT([a1, z1], T.WB[:, XV:2 * XV], T.WB[:, 0:XV], F.Silu)
+    a5 = ACT([], T.WB[:, 2 * XV:XA], T.WB[:, 0:XA - 2 * XV], F.Silu)
     V([], "ms", T.WA[:, 2048:5120], 0.0)
+    v_pb = V([], "ts", T.pb[:], T.pti[:], 16.0, 16.0, A.mult, A.add)
     v_nls = V([l_nxt], "cp", T.nls[:], T.nxi[:])
     v_wa = V([], "ms", T.WA[:, 5120:8192], 0.0)
-    DMA("s", "dda", [v_da, c_lta], T.DA[1::16, :], T.ltA[:])
-    DMA("s", "ddb", [v_db, a2, c_ltb], T.DB[1::16, :], T.ltB[:])
-    DMA("s", "ddb", [v_pfb], T.DB[2::16, :], T.pfB[:])
-    d_b = DMA("s", "ddb", [a_htb], T.DB[0::16, :], T.htB[:])
-    DMA("s", "dda", [a_hta], T.DA[0::16, :], T.htA[:])
-    d_a = DMA("s", "dda", [v_pb], T.DA[2::16, :], T.pb[:, 0:128])
-    DMA("s", "dprow", [], T.prow[:, 0:2048], T.pb[:, 0:128])
-    d_prow = DMA("s", "dprow", [], T.prow[:, 2048:4096], T.pb[:, 128:256])
 
-    IOTA([], T.WB[:, 5248:6720], [[0, 1472]], 0, 0)
-    p_z2 = IOTA([], T.WB[:, 6720:8192], [[0, 1472]], 0, 0)
-    r_n = SEND([v_nls], nxc, T.nl[:], T.nls[:], "rn")
-    p_z = IOTA([], T.BZ[:], [[0, 704]], 0, 0)
+    IOTA([], T.WB[:, XA:XA + XP1], [[0, XP1]], 0, 0)
+    r_p = SEND([v_pf], opp, T.pf[:], T.pfs[:], "rp", 2)
+    r_o = SEND([v_ols], opp, T.ol[:], T.ols[:], "ro", 2)
+    p_z2 = IOTA([], T.WB[:, XA + XP1:8192], [[0, 8192 - XA - XP1]], 0, 0)
+    r_n = SEND([v_nls], prv, T.nl[:], T.nls[:], "rn")
+    p_z = IOTA([], T.BZ[:], [[0, 424]], 0, 0)
 
-    s_b = ACT([a5, p_z2, v_ol, d_b], T.WB[:].indirect(T.ol[:, 128:256]), T.DB[:], F.Silu)
-    s_a = V([v_wa, v_ol, d_a], "cp", T.WA[:].indirect(T.ol[:, 0:128]), T.DA[:])
+    d_d = DMA("s", "dd", [r_p, a_d], T.D[2::8, :], T.pf[:])
+    d_prow = DMA("s", "dprow", [v_pb], T.prow[:], T.pb[:])
 
-    BI, B2, B0, B8 = ((T.BZ, 144 * k) for k in range(4))
-    ID = T.BZ[:, 576:704]
+    s_b = ACT([a5, p_z2, r_o, d_d], T.WB[:].indirect(T.ol[:, 128:256]), T.D[:], F.Silu)
+    s_a = V([v_wa, r_o, d_d], "cp", T.WA[:].indirect(T.ol[:, 0:128]), T.D[:])
+
+    BI, B8 = (T.BZ, 0), (T.BZ, 144)
+    ID = T.BZ[:, 288:416]
+    B2 = T.BZ[:, 416:424]
     E = (T.BO, 0)
-    E256 = (T.E4, 0)
     LS = T.BO[:, 144:272]
     SG = T.BO[:, 272:400]
 
-    def rowsel(mat, fills):
-        buf = mat[0][:, mat[1]:mat[1] + 144]
-        tok = p_z
-        for k, w in fills:
-            tok = SEL([tok], buf, [[-16, 9], [0, 16]], A.not_equal, w, -k, 1)
-        return SEL([tok], buf, [[0, 9], [1, 16]], A.is_equal, 0.0, -15, 0)
-
-    m_bi = rowsel(BI, [(0, 8.0), (1, 0.0625)])
-    m_b8 = SEL([p_z], T.BZ[:, 432:576], [[-1, 144]], A.not_equal, 0.0625, 15, 16)
-    m_b2 = rowsel(B2, [(2, 0.0625)])
+    m_b8 = SEL([p_z], T.BZ[:, 144:288], [[-1, 144]], A.not_equal, 0.0625, 15, 16)
+    m_bi = m_b2 = p_z
+    for k, w in ((0, 4.0), (8, 4.0), (1, -0.0625), (9, -0.0625)):
+        m_bi = SEL([m_bi], T.BZ[:, 0:144], [[-16, 9], [-256, 16]], A.not_equal, w, 3840 - k, 1)
+    for k in (2, 10):
+        m_b2 = SEL([m_b2], B2, [[-16, 8]], A.not_equal, -0.0625, -k, 1)
     IOTA([], T.R[:, 4096:4112], [[0, 16]], 0, 0)
-    IOTA([], T.V2[:, 4096:4112], [[0, 16]], 0, 0)
     v_zx = IOTA([], T.zx[:], [[0, 32]], 0, 0)
     m_id = SEL([p_z], ID, [[-1, 128]], A.not_equal, 1.0, 0, 1)
     IOTA([], T.BO[:, 128:144], [[0, 16]], 0, 0)
     p_one = IOTA([], SG, [[0, 128]], 1, 0)
+    m = SEL([p_one], SG, [[-16, 8], [0, 16]], A.is_ge, 0.0, 0, 1)
+    m_sg = SEL([m], SG, [[16, 8], [0, 16]], A.is_ge, 0.0, 15, -1)
+    m_e = SELO([m_sg], T.BO[:, 0:128], SG, [[0, 8], [1, 16]], A.is_equal, -15, 0)
+    m_ls = SELO([m_sg], LS, SG, [[1, 128]], A.is_gt, 0, -1)
 
     MM([m_b8, d_prow], rewrap(T.b7[:, 0:128], B8, T.prow, 0, 128, 8, False)
        + rewrap(T.b5[:, 0:128], B8, T.prow, 128, 256, 8, False), False)
 
     def tlist(out, src, c0, c1):
-        return [(out[0:c1 - c0, t:128:16], src[:, 16 * c0 + t:16 * c1:16], T.BZ[:, 159:287:16], True, True)
-                for t in range(16)]
+        return [(out[0:c1 - c0, t:128:16], src[:, 16 * c0 + t:16 * c1:16], B2, True, True) for t in range(16)]
 
-    g_a = [ACT([s_b, r_n], el(T.bg, c0, c1), T.WB[:].indirect(T.nl[:, c0:c1]), F.Copy) for c0, c1 in SUBS]
+    IOTA([], T.K[:], [[4095, 2], [-4097, 2]], 1, 0)
+    IOTA([], T.K2[:], [[-4096, 2], [-4095, 2]], 4096, 0)
+    IOTA([], T.e1[:], [[1, 17]], 1025, 17)
+    IOTA([], T.pr[:], [[16, 16], [1, 18]], 0, 0, False)
+    IOTA([], T.cv[:], [[1, 272]], 0, 0)
+
+    g_a = [ACT([s_b, r_n], el(T.bg, c0, c1), T.WB[:].indirect(T.nl[:, c0:c1]), F.Copy, None, -1.0) for c0, c1 in SUBS]
     upto = {}
     t_code = [None] * 4
     v_jl = [None] * 4
+    r_x = [None] * 4
 
     def jl(q):
-        v_jl[q] = V([t_code[q]], "ts", T.jl[:, 64 * q:64 * q + 64], T["b%d" % q][:, 0:64], -1.0, 4096.0, A.mult, A.add)
+        cols = slice(64 * q, 64 * q + 64)
+        v_jl[q] = V([t_code[q]], "ts", T.jl[:, cols], T["b%d" % q][:, 0:64], 4096.0, None, A.add)
+        r_x[q] = SEND([v_jl[q]], nxc, T.jx[:, cols], T.jl[:, cols], "rx%d" % q)
 
-    r_y, r_x = [], []
     for k, (c0, c1) in enumerate(SUBS):
-        upto[c1] = V([s_a, g_a[k], r_n], "tt", el(T.R, c0, c1), T.WA[:].indirect(T.nl[:, c0:c1]), el(T.bg, c0, c1), A.add)
-        for s0, s1 in SENDS:
-            if s1 == c1:
-                r_v = SEND([upto[c1]], opp, el(T.V2, s0, s1), el(T.R, s0, s1), "rv")
+        upto[c1] = V([s_a, g_a[k], r_n], "tt", el(T.R, c0, c1), T.WA[:].indirect(T.nl[:, c0:c1]), el(T.bg, c0, c1), A.min)
         if c1 % 64 == 0:
             q = c1 // 64 - 1
             t_code[q] = MM([upto[c1], m_bi], rewrap(T["b%d" % q][:, 0:64], BI, T.R, 64 * q, 64 * q + 64))
             if q == 1:
                 MM([m_b2], tlist(T.b6[:, 0:128], T.R, 0, 128), False)
-        if c1 == 32:
-            m = SEL([p_one], SG, [[-16, 8], [0, 16]], A.is_ge, 0.0, 0, 1)
-        if c1 == 96:
-            m_sg = SEL([m], SG, [[16, 8], [0, 16]], A.is_ge, 0.0, 15, -1)
+        if c1 in (128, 192, 256):
+            jl(c1 // 64 - 2)
         if c1 == 128:
-            jl(0)
-            r_y.append(SEND([v_jl[0]], nxc, T.jy[:, 0:64], T.jl[:, 0:64], "ry0"))
-        if c1 == 160:
-            m_e = SELO([m_sg], T.BO[:, 0:128], SG, [[0, 8], [1, 16]], A.is_equal, -15, 0)
-        if c1 == 192:
-            jl(1)
-            r_y.append(SEND([v_jl[1]], nxc, T.jy[:, 64:NY], T.jl[:, 64:NY], "ry1"))
-        if c1 == 240:
-            jl(2)
-            r_x.append(SEND([v_jl[2]], prv, T.jx[:, 0:192 - NY], T.jl[:, NY:192], "rx0"))
-
-    gy2 = []
-    for r, (c0, cm, c1) in zip(r_y, ((0, 32, 64), (64, 96, NY))):
-        gy2.append(V([upto[256], r, v_zx], "cp", el(T.R2y, c0, cm), T.R[:].indirect(T.jy[:, c0:cm])))
-        gy2.append(ACT([upto[256], r, v_zx], el(T.R2y, cm, c1), T.R[:].indirect(T.jy[:, cm:c1]), F.Copy))
-        if c0 == 0:
-            v_owf = V([l_own], "cp", T.owf[:], T.owi[:])
-            jl(3)
-            r_x.append(SEND([v_jl[3]], prv, T.jx[:, 192 - NY:256 - NY], T.jl[:, 192:256], "rx1"))
-    c_ci = IOTA([], T.ci[:], [[1, 16]], 1025, 0)
-    t_kf = MM([m_b2], tlist(T.b6[:, 128:256], T.R, 128, 256))
-    a_kf = ACT([t_kf], T.kfs[:], T.b6[:, 0:256], F.Copy)
-    r_f = SEND([a_kf], prv, T.kfl[:], T.kfs[:], "rf")
-    t_ky = MM(gy2 + [v_jl[0]], tlist(T.b0, T.R2y, 0, NY))
-    a_ky = ACT([t_ky], T.kYs[:], T.b0[:, 0:128], F.Copy)
-    r_k = SEND([a_ky], opp, T.kYl[:], T.kYs[:], "rk")
-    p_ones = IOTA([], T.ones[:], [[0, 256]], 1, 0)
-    c_d3 = IOTA([], T.d3[:], [[16, 16], [256, 16]], 0, 0)
-    m_ls = SELO([m_sg], LS, SG, [[1, 128]], A.is_gt, 0, -1)
-    m_nl = SELO([m_sg], T.NL[:], SG, [[-1, 128]], A.is_gt, 0, 1)
-    m_b0 = rowsel(B0, [(0, 0.0625)])
-    c_mi = IOTA([], T.mi[:], [[1, 512]], 0, 0)
+            c_late = IOTA([], T.d0[:], [[0, 512]], -1, 0)
+    DMA("s", "dk", [c_late], T.K[0::16, :], T.K2[0:8, :])
+    DMA("s", "dk", [], T.pri[:], T.pr[:])
+    DMA("s", "dk", [], T.e1[15::16, 16:17], T.K2[0:8, 2:3])
+    d_k = DMA("s", "dk", [], T.d0[0::16, :], T.zx[:])
+    DMA("s", "dwin", [d_k, g_a[-1]], T.WB[0::16, 4096:4097], T.K[1:9, 3:4])
+    DMA("s", "dwin", [], T.WB[1::16, 4096:4097], T.K2[0:8, 2:3])
 
     def gx(c0, c1):
-        return el(T.R2x, c0 - NY, c1 - NY), T.V2[:].indirect(T.jx[:, c0 - NY:c1 - NY])
+        return el(T.R2, c0, c1), T.R[:].indirect(T.jx[:, c0:c1])
 
-    g1 = [V([r_v, r_x[0], v_zx], "cp", *gx(128, 164)), ACT([r_v, r_x[0], v_zx], *gx(164, 192), F.Copy)]
-    g2 = [V([r_x[1]], "cp", *gx(192, 224)), ACT([r_x[1]], *gx(224, 256), F.Copy)]
-    DMA("s", "dwin", [v_owf, g_a[-1], g2[1]], T.WB[0::16, 0:4096], T.owf[:])
+    row = [upto[256], v_zx]
+    g1 = [ACT(row + [r_x[1]], *gx(64, 128), F.Copy), V(row + [r_x[0]], "cp", *gx(0, 44))]
+    jl(3)
+    g1.append(V([], "cp", *gx(44, 64)))
+    t_kf = MM([m_b2], tlist(T.b6[:, 128:256], T.R, 128, 256))
+    g2 = [V([r_x[2]], "cp", *gx(128, 164)), ACT([r_x[2]], *gx(164, 192), F.Copy)]
+    a_kf = ACT([t_kf], T.kfs[:], T.b6[:, 0:256], F.Copy)
+    r_f = SEND([a_kf], nxc, T.kfl[:], T.kfs[:], "rf")
+    t_k0 = MM(g1 + [v_jl[0]], tlist(T.b0, T.R2, 0, 128))
 
-    def back(bank, c0, c1, kt):
-        n = c1 - c0
-        return [(bank[:, 0:n], kt[0:n, :], ID[0:n, 0:n], True, True)]
+    def back(bank, p):
+        return [(bank[:, 0:128], T.kX[:, 128 * p:128 * p + 128], ID, True, True)]
 
     def plus(bank, kt, last):
         return [(bank[:, 0:128], kt, ID, False, last)]
 
-    def kept(bank, c0, c1, tok):
-        return V([tok], "ts", T.kept[:, c0:c1], bank[:, 0:c1 - c0], 0.5, None, A.is_gt)
+    def kept(bank, p, tok):
+        return V([tok], "ts", T.kept[:, 128 * p:128 * p + 128], bank[:, 0:128], 0.5, None, A.is_gt)
 
     def zsum(s0, s1, first, last):
         return [(T.b4[:, 0:16], moved(E, s), T.kept[:, 16 * s:16 * s + 16], first and s == s0, last and s == s1 - 1)
                 for s in range(s0, s1)]
 
-    MM([r_f, m_id], plus(T.b7, T.kfl[:, 0:128], False) + plus(T.b5, T.kfl[:, 128:256], False), False)
-    t_k1 = MM(g1 + g2 + [v_jl[1]], tlist(T.b1, T.R2x, 0, 128))
-    v_padc = V([], "ts", T.padc[:], T.pm[:], 0.5, -1.0, A.is_lt, A.mult)
-    v_cc = V([], "ts", T.ccol[:], T.pm[:], 16.0, None, A.mult)
-    v_cst = V([v_cc, c_ci], "ts", T.cst[:], T.ci[:], T.ccol[:], None, A.add)
-    t_by = MM([r_k, v_jl[3], m_id], back(T.b3, 0, NY, T.kYl))
-    t_y0 = MM([], plus(T.b7, T.kYl[:], True))
-    a_k1 = ACT([t_k1], T.kX1[:], T.b1[:, 0:128], F.Copy)
-    c_mk = ACT([], T.mk[:, 0:1024], T.V2[:, 0:1024], F.Copy, None, 0.0)
-    v_cy = kept(T.b3, 0, NY, t_by)
-    t_b1 = MM([a_k1], back(T.b0, 128, 256, T.kX1))
-    MM([v_cy, m_e], zsum(0, 8, True, False), False)
-    v_c1 = kept(T.b0, 128, 256, t_b1)
-    v_e4 = V([m_e], "ts", T.E4[:], T.BO[:, 0:144], 256.0, None, A.mult)
-    t_z = MM([v_c1, v_jl[2]], zsum(8, 16, False, True))
-    v_zc = V([t_z, v_zx, v_cst, p_ones], "scan", T.zx[:, 1:17], T.ones[:, 0:16], T.b4[:, 0:16], 0.0, A.mult, A.add)
-    t_y1 = MM([], plus(T.b5, T.kX1[:], True))
-    ACT([t_y0], T.YW[:, 0:128], T.b7[:, 0:128], F.Identity, -3.0)
-    a_yw = ACT([t_y1], T.YW[:, 128:256], T.b5[:, 0:128], F.Identity, -3.0)
-    DMA("s", "dwin", [a_yw], T.WB[1::16, 0:4096], T.YW[:])
-    t_off = MM([v_zc, m_ls], [(T.b1[:, 128:129], LS, T.zx[:, 16:17], True, True)])
-    v_e0 = V([t_z], "ts", T.e0[:], T.b4[:, 0:16], 0.0, None, A.is_equal)
-    v_e1 = V([v_e0, v_cst], "tt", T.e1[:], T.e0[:], T.cst[:], A.mult)
-    v_p1 = V([v_e1, v_zc], "tt", T.p1[:], T.e1[:], T.zx[:, 0:16], A.add)
-    v_zl = V([v_p1, t_off], "ts", T.zl[:], T.p1[:], T.b1[:, 128:129], None, A.add)
-    MM([m_sg], [(T.b3[:, 0:256], SG, T.kept[:], True, True)], False)
-    t_n1 = MM([m_nl], [(T.b3[:, 256:512], T.NL[:], T.kept[:], True, True)])
-    v_pad = ACT([v_padc, c_mk], T.WB[:, 4096:4352], T.mk[:, 0:256], F.Identity, T.padc[:])
-    v_mks = V([v_zl, c_mk, v_pad, c_d3], "cp", T.mk[:].indirect(T.zl[:]), T.d3[:])
-    v_b0 = V([v_mks], "scan", T.blk[:, 0:512], T.mk[:, 0:512], T.mk[:, 0:512], 0.0, A.max, A.max)
-    v_b1 = V([v_b0], "scan", T.blk[:, 512:1024], T.mk[:, 512:1024], T.mk[:, 512:1024], T.blk[:, 511:512], A.max, A.max)
-    t_bl = [MM([v_b, m_b0], rewrap(b[:, 0:32], B0, T.blk, 32 * h, 32 * h + 32))
-            for h, (v_b, b) in enumerate(((v_b0, T.b0), (v_b1, T.b1)))]
-    v_cum = V([t_n1], "scan", T.cum[:], T.ones[:], T.b3[:, 0:256], 0.0, A.mult, A.add)
-    v_kw = V([v_cum], "tt", T.KW[:], T.cum[:], T.b3[:, 256:512], A.subtract)
-    a_kv = ACT([v_kw], T.KV[:], T.KW[:], F.Identity, -512.0)
-    v_bl, v_hit = [], []
-    for h, (b, kw, tok) in enumerate(((T.b0, T.KW, v_kw), (T.b1, T.KV, a_kv))):
-        lst = T.bl[:, 32 * h:32 * h + 32]
-        v_bl.append(V([t_bl[h]], "cp", lst, b[:, 0:32]))
-        v_hit.append(V([tok, v_bl[h], c_mi], "tt", T.hit[:, 512 * h:512 * h + 512], kw[:].indirect(lst), T.mi[:], A.is_le))
-    t_h = []
-    for h, (b, o) in enumerate(((T.b0, T.b2), (T.b1, T.b6))):
-        a_bc = ACT([v_bl[h]], T.blc[:, 32 * h:32 * h + 32], b[:, 0:32], F.Copy)
-        MM([a_bc], [(o[:, 0:32], ID, T.blc[:, 32 * h:32 * h + 32], True, False)], False)
-        t_h.append(MM([v_hit[h], v_e4], rewrap(o[:, 0:32], E256, T.hit, 32 * h, 32 * h + 32, first=False)))
-    v_of = [V([t_h[h]], "cp", T.off[:, 32 * h:32 * h + 32], o[:, 0:32]) for h, o in enumerate((T.b2, T.b6))]
-    win = T.WB[:, 0:4352]
-    rows = [v_pad, ("dwin", cnt["dwin"])]
-    ACT([v_of[0]] + rows, T.res[:, 0:512], win.indirect(T.off[:, 0:32]), F.Copy)
-    v_r = V([v_of[1]] + rows, "cp", T.res[:, 512:768], win.indirect(T.off[:, 32:48]))
-    a_r = ACT([v_of[1]], T.res[:, 768:1024], win.indirect(T.off[:, 48:64]), F.Copy)
+    def column(bank, c0, n):
+        return [(bank[:, 0:n], moved(E, 0), T.cv[:, c0:c0 + n], True, False)]
+
+    def before(bank, c0):
+        return [(bank[:, 0:128], LS, T.kept[:, c0:c0 + 128], False, True)]
+
+    a_k0 = ACT([t_k0], T.kX[:, 0:128], T.b0[:, 0:128], F.Copy)
+    g2.append(V([r_x[3]], "cp", *gx(192, 228)))
+    g2.append(ACT([r_x[3]], *gx(228, 256), F.Copy))
+    t_b0 = MM([a_k0, v_jl[2], m_id], back(T.b2, 0))
+    MM([a_kf, c_late, m_e], column(T.b0, 0, 128) + column(T.b6, 128, 144), False)
+    v_c0 = kept(T.b2, 0, t_b0)
+    t_k1 = MM(g2 + [v_jl[1]], tlist(T.b1, T.R2, 128, 256))
+    v_owf = V([l_own], "cp", T.owf[:], T.owi[:])
+    DMA("s", "dwin", [v_owf], T.WB[0::16, 0:4096], T.owf[:])
+    v_perm = V([d_k], "cp", T.swp[:], T.pri[:])
+    V([], "ms", T.mk[:, 384:1024], 0.0)
+    ACT([], T.mk[:, 0:384], T.R[:, 0:384], F.Copy, None, 0.0)
+    a_k1 = ACT([t_k1], T.kX[:, 128:256], T.b1[:, 0:128], F.Copy)
+    MM([v_c0, m_e, m_ls], zsum(0, 4, True, False), False)
+    t_b1 = MM([a_k1, v_jl[3]], back(T.b3, 1))
+    t_l0 = MM([], before(T.b0, 0))
+    MM([], zsum(4, 8, False, False), False)
+    v_c1 = kept(T.b3, 1, t_b1)
+    ACT([t_l0], T.loc[:, 0:128], T.b0[:, 0:128], F.Copy)
+    t_l1 = MM([v_c1], before(T.b6, 128))
+    t_z = MM([], zsum(8, 16, False, True))
+    a_loc = ACT([t_l1], T.loc[:, 128:272], T.b6[:, 0:144], F.Copy)
+    a_dt = ACT([a_loc, v_perm], T.DT[:], T.loc[:].indirect(T.swp[:, 0:17]), F.Copy)
+    v_zc = V([t_z, d_k], "scan", T.zx[:, 1:17], T.R[:, 4096:4112], T.b4[:, 0:16], 0.0, A.add, A.add)
+    t_off = MM([v_zc], [(T.b1[:, 128:129], LS, T.zx[:, 16:17], True, True)])
+    t_y = MM([r_f], plus(T.b7, T.kfl[:, 0:128], False) + plus(T.b5, T.kfl[:, 128:256], False)
+             + plus(T.b7, T.kX[:, 0:128], True) + plus(T.b5, T.kX[:, 128:256], True))
+    ACT([t_y], T.YW[:, 0:128], T.b7[:, 0:128], F.Identity, -3.0)
+    a_yw = ACT([], T.YW[:, 128:256], T.b5[:, 0:128], F.Identity, -3.0)
+    d_win = DMA("s", "dwin", [a_yw], T.WB[1::16, 0:4096], T.YW[:])
+    v_e0 = V([d_k], "ts", T.e0[:], T.b4[:, 0:16], 0.0, None, A.is_equal)
+    v_e1 = V([v_e0], "tt", T.e1[:, 0:16], T.e0[:], T.e1[:, 0:16], A.mult)
+    v_p1 = V([v_e1, v_zc], "tt", T.p1[:], T.e1[:], T.zx[:, 0:17], A.add)
+    v_zl = V([v_p1, t_off], "ts", T.zl[:, 0:17], T.p1[:], T.b1[:, 128:129], None, A.add)
+    v_mks = V([v_zl, a_dt], "cp", T.mk[:].indirect(T.zl[:, 0:17]), T.DT[:])
+    v_s0 = V([v_mks], "scan", T.S[:, 0:512], T.d0[:], T.mk[:, 0:512], 0.0, A.add, A.max)
+    v_s1 = V([v_s0], "scan", T.S[:, 512:1024], T.d0[:], T.mk[:, 512:1024], T.S[:, 511:512], A.add, A.max)
+    a_h = ACT([v_s0], T.hit[:, 0:512], T.S[:, 0:512], F.Relu, T.K[:, 2:3], T.K[:, 1:2])
+    v_h = V([v_s1], "ts", T.hit[:, 512:1024], T.S[:, 512:1024], T.K[:, 0:1], T.K[:, 1:2], A.min, A.mult)
+    t_h = MM([a_h, v_h], rewrap(T.b2[:, 0:64], E, T.hit, 0, 64))
+    v_o0 = V([t_h], "ts", T.off[:, 0:32], T.b2[:, 0:32], 0.0625, None, A.mult)
+    v_o1 = V([], "ts", T.off[:, 32:64], T.b2[:, 32:64], 0.0625, 3840.0, A.mult, A.add)
+    win = T.WB[:, 0:4112]
+    a_r = ACT([v_o0, d_win], T.res[:, 0:512], win.indirect(T.off[:, 0:32]), F.Copy)
+    v_r = V([v_o1, d_win], "cp", T.res[:, 512:1024], win.indirect(T.off[:, 32:64]))
     DMA("s", "dout", [a_r, v_r], T.yk[:], T.res[0::16, :])
     DMA("a", "dout", [a_r, v_r], T.ys[:], T.res[1::16, :])
     need("p", [(s, cnt[s]) for s in sorted(cnt)])

@@ -8,16 +8,16 @@ SCRATCH = {
     "ol": ("sbuf", [128, 256], "uint16"),
     "pfs": ("sbuf", [128, 256], "float32"),
     "pf": ("sbuf", [128, 256], "float32"),
+    "pb": ("sbuf", [128, 256], "bfloat16"),
     "nls": ("sbuf", [128, 256], "uint16"),
     "nl": ("sbuf", [128, 256], "uint16"),
-    "pb": ("sbuf", [128, 256], "bfloat16"),
     "jl": ("sbuf", [128, 256], "uint16"),
     "jx": ("sbuf", [128, 256], "uint16"),
     "D": ("sbuf", [128, 2048], "float32"),
     "WA": ("sbuf", [128, 8192], "bfloat16"),
     "WB": ("sbuf", [128, 8192], "float32"),
     "bg": ("sbuf", [128, 4096], "bfloat16"),
-    "R": ("sbuf", [128, 4112], "bfloat16"),
+    "R": ("sbuf", [128, 4240], "bfloat16"),
     "R2": ("sbuf", [128, 4096], "bfloat16"),
     "prow": ("sbuf", [8, 4096], "bfloat16"),
     "pid": ("sbuf", [128, 1], "int32"),
@@ -26,30 +26,29 @@ SCRATCH = {
     "s16": ("sbuf", [128, 1], "float32"),
     "sc": ("sbuf", [128, 1], "float32"),
     "ev": ("sbuf", [128, 1], "float32"),
+    "u4": ("sbuf", [128, 1], "float32"),
     "jj": ("sbuf", [128, 8], "float32"),
     "hb": ("sbuf", [128, 8], "float32"),
     "xx": ("sbuf", [128, 256], "float32"),
-    "pr": ("sbuf", [8, 288], "int32"),
-    "pri": ("sbuf", [128, 18], "int32"),
     "K": ("sbuf", [128, 4], "float32"),
     "K2": ("sbuf", [128, 4], "float32"),
-    "swp": ("sbuf", [128, 18], "uint16"),
-    "BZ": ("sbuf", [128, 424], "bfloat16"),
-    "BO": ("sbuf", [128, 400], "bfloat16"),
+    "BZ": ("sbuf", [128, 1000], "bfloat16"),
+    "Q": ("sbuf", [128, 4, 17], "bfloat16"),
+    "lo": ("sbuf", [128, 17], "bfloat16"),
+    "c2": ("sbuf", [128, 64], "bfloat16"),
+    "msk": ("sbuf", [128, 384], "bfloat16"),
+    "PM": ("sbuf", [128, 512], "bfloat16"),
+    "L": ("sbuf", [128, 256], "bfloat16"),
     "cv": ("sbuf", [128, 272], "bfloat16"),
     "d0": ("sbuf", [128, 512], "bfloat16"),
-    "mk": ("sbuf", [128, 4240], "bfloat16"),
+    "mk": ("sbuf", [128, 5376], "bfloat16"),
     "S": ("sbuf", [128, 1024], "bfloat16"),
     "hit": ("sbuf", [128, 1024], "bfloat16"),
     "off": ("sbuf", [128, 64], "uint16"),
     "kX": ("sbuf", [128, 256], "bfloat16"),
     "kfs": ("sbuf", [128, 256], "bfloat16"),
     "kfl": ("sbuf", [128, 256], "bfloat16"),
-    "kept": ("sbuf", [128, 256], "bfloat16"),
-    "loc": ("sbuf", [128, 272], "bfloat16"),
     "DT": ("sbuf", [128, 272], "bfloat16"),
-    "zx": ("sbuf", [128, 32], "bfloat16"),
-    "e0": ("sbuf", [128, 16], "float32"),
     "e1": ("sbuf", [128, 17], "float32"),
     "p1": ("sbuf", [128, 17], "float32"),
     "zl": ("sbuf", [128, 18], "uint16"),
@@ -59,11 +58,12 @@ SCRATCH = {
 }
 for _k in range(8):
     SCRATCH["b%d" % _k] = ("psum", [128, 512], "float32")
-SEMAPHORES = ["v", "a", "t", "p", "down", "dpts", "dnxt", "dd", "dprow", "dk", "dwin", "dout",
-              "rp", "ro", "rn", "rx0", "rx1", "rx2", "rx3", "rf", "sent"]
+SEMAPHORES = ["v", "a", "t", "p", "down", "dpts", "dnxt", "dd", "dz", "dprow", "dk", "dq", "dwin", "dout",
+              "rp", "ro", "rn", "rx1", "rx2", "rx3", "rf", "sent"]
 
-SUBS = [(0, 16), (16, 32)] + [(k, k + 32) for k in range(32, 224, 32)] + [(224, 240), (240, 256)]
-XV, XA, XP1 = 2176, 6272, 512
+SUBS = [(k, k + 32) for k in range(0, 256, 32)]
+XZ, XA, XV, XP1, XP2 = 1024, 5600, 5908, 512, 192
+NV = 4
 
 
 def rank_program(g, core, T, topo):
@@ -141,10 +141,10 @@ def rank_program(g, core, T, topo):
             ins = g.tensor.matmul(out, lhs, rhs, st, sp)
         return done("t", ins, 1) if tok else None
 
-    def SEND(toks, to, dst, src, sem, step=1):
+    def SEND(toks, to, dst, src, sem, part=slice(None)):
         need("p", toks)
         rid, pid, _se = topo.addr(to)
-        engines = topo.engines(core, to)[::step]
+        engines = topo.engines(core, to)[part]
         g.remote_dma(out_ap=dst, in_ap=src, remote_sem=T.sem[sem], local_sem=T.sem.sent, pid=pid, routing_id=rid,
                      dma_engine_mask=sum(1 << e for e in engines))
         n = len(engines)
@@ -156,199 +156,212 @@ def rank_program(g, core, T, topo):
         buf, c = mat
         return buf[0:K, c + 15 - t:c + 143 - t]
 
-    def rewrap(out, mat, src, c0, c1, K=128, close=True, first=True):
-        return [(out, moved(mat, t, K), src[0:K, 16 * c0 + t:16 * c1:16], first and t == 0, close and t == 15)
-                for t in range(16)]
+    def rewrap(out, mat, src, c0, c1, K=128, close=True):
+        return [(out, moved(mat, t, K), src[0:K, 16 * c0 + t:16 * c1:16], t == 0, close and t == 15) for t in range(16)]
 
     def el(buf, c0, c1):
         return buf[:, 16 * c0:16 * c1]
 
-    l_pts = DMA("s", "dpts", [], T.pti[:], T.pts[:])
     l_own = DMA("s", "down", [], T.owi[:], T.own[:])
+    l_pts = DMA("s", "dpts", [], T.pti[:], T.pts[:])
     l_nxt = DMA("s", "dnxt", [], T.nxi[:], T.nxt[:])
 
     c_pid = IOTA([], T.pid[:], [[1, 1]], 0, 1, False)
     c_j = IOTA([], T.jj[:], [[-4, 8]], 48, 0)
     c_x = IOTA([], T.xx[:], [[1, 256]], 0, 0)
     z0 = V([], "ms", T.WB[:, 0:64], 0.0)
+    z1 = V([], "ms", T.WB[:, 128:XZ], 0.0)
     v_h8 = V([c_pid], "ts", T.h8[:], T.pid[:], 8, None, A.bitwise_and)
-    v_o1 = V([], "ts", T.o1[:], T.pid[:], 1, None, A.bitwise_and)
+    v_o1 = V([], "ts", T.o1[:], T.pid[:], 5, None, A.bitwise_and)
     v_s = V([v_h8], "ts", T.s16[:], T.h8[:], 4.0, -16.0, A.mult, A.add)
-    V([], "ms", T.WA[:, 0:256], 0.0)
-    v_sc = V([v_s, v_o1], "ts", T.sc[:], T.o1[:], T.s16[:], None, A.mult)
-    V([], "ms", T.WA[:, 256:512], 0.0)
+    v_sc = V([v_s, v_o1], "ts", T.sc[:], T.o1[:], 1.0, T.s16[:], A.is_equal, A.mult)
+    V([], "ts", T.u4[:], T.o1[:], -4.0, T.s16[:], A.mult, A.add)
     v_ev = V([v_sc], "ts", T.ev[:], T.s16[:], T.sc[:], None, A.subtract)
-    V([], "ms", T.WA[:, 512:768], 0.0)
-    v_bias = V([v_ev, c_j], "ts", T.hb[:], T.jj[:], T.s16[:], T.ev[:], A.subtract, A.mult)
-    V([], "ms", T.WA[:, 768:1536], 0.0)
-    v_pf = V([l_pts], "ts", T.pfs[:], T.pti[:], 1.0, T.s16[:], A.add, A.mult)
-    V([], "ms", T.WA[:, 1536:2048], 0.0)
     v_ols = V([l_own], "cp", T.ols[:], T.owi[:])
-    z1 = V([], "ms", T.WB[:, 128:XV], 0.0)
-    a1 = ACT([z0], T.WB[:, 64:128], T.WB[:, 0:64], F.Silu)
+    v_bias = V([v_ev, c_j], "ts", T.hb[:], T.jj[:], T.u4[:], T.ev[:], A.subtract, A.mult)
+    V([], "ms", T.WA[:, 0:384], 0.0)
+    v_pf = V([l_pts], "ts", T.pfs[:], T.pti[:], 1.0, T.s16[:], A.add, A.mult)
+    a5 = ACT([z0], T.WB[:, 64:128], T.WB[:, 0:64], F.Silu)
+    a5 = ACT([a5, z1], T.WB[:, XZ:2 * XZ], T.WB[:, 0:XZ], F.Silu)
     for j in range(8):
-        a_d = ACT([v_bias, c_x], T.D[:, 256 * j:256 * j + 256], T.xx[:], F.Identity, T.hb[:, j:j + 1], T.sc[:])
-    ACT([a1, z1], T.WB[:, XV:2 * XV], T.WB[:, 0:XV], F.Silu)
-    a5 = ACT([], T.WB[:, 2 * XV:XA], T.WB[:, 0:XA - 2 * XV], F.Silu)
-    V([], "ms", T.WA[:, 2048:5120], 0.0)
+        out = T.D[:, 256 * j:256 * j + 256]
+        if j < NV:
+            v_d = V([v_bias, c_x], "ts", out, T.xx[:], T.sc[:], T.hb[:, j:j + 1], A.mult, A.add)
+        else:
+            a_d = ACT([v_bias, c_x], out, T.xx[:], F.Identity, T.hb[:, j:j + 1], T.sc[:])
+    for c in range(2 * XZ, XA, 2 * XZ):
+        a_wb = ACT([a5], T.WB[:, c:min(c + 2 * XZ, XA)], T.WB[:, 0:min(2 * XZ, XA - c)], F.Silu)
+    v_wa0 = V([], "ms", T.WA[:, 384:768], 0.0)
     v_pb = V([], "ts", T.pb[:], T.pti[:], 16.0, 16.0, A.mult, A.add)
+    v_wb = V([], "ms", T.WB[:, XA:XV], 0.0)
     v_nls = V([l_nxt], "cp", T.nls[:], T.nxi[:])
-    v_wa = V([], "ms", T.WA[:, 5120:8192], 0.0)
+    v_wa = V([], "ms", T.WA[:, 768:8192], 0.0)
 
-    IOTA([], T.WB[:, XA:XA + XP1], [[0, XP1]], 0, 0)
-    r_p = SEND([v_pf], opp, T.pf[:], T.pfs[:], "rp", 2)
-    r_o = SEND([v_ols], opp, T.ol[:], T.ols[:], "ro", 2)
-    p_z2 = IOTA([], T.WB[:, XA + XP1:8192], [[0, 8192 - XA - XP1]], 0, 0)
-    r_n = SEND([v_nls], prv, T.nl[:], T.nls[:], "rn")
-    p_z = IOTA([], T.BZ[:], [[0, 424]], 0, 0)
+    def clear(c0, c1):
+        return IOTA([], T.WB[:, c0:c1], [[0, c1 - c0]], 0, 0)
 
-    d_d = DMA("s", "dd", [r_p, a_d], T.D[2::8, :], T.pf[:])
+    clear(XV, XV + XP1)
+    r_o = SEND([v_ols], opp, T.ol[:], T.ols[:], "ro", slice(1, None, 4))
+    clear(XV + XP1, XV + XP1 + XP2)
+    r_p = SEND([v_pf], opp, T.pf[:], T.pfs[:], "rp", slice(0, None, 2))
+    p_z2 = clear(XV + XP1 + XP2, 8192)
+
+    d_d = DMA("s", "dd", [r_p, a_d, v_d], T.D[2::8, :], T.pf[:])
+    p_z = DMA("s", "dz", [v_wa0], T.BZ[:, 0:744], T.WA[:, 0:744])
     d_prow = DMA("s", "dprow", [v_pb], T.prow[:], T.pb[:])
 
-    s_b = ACT([a5, p_z2, r_o, d_d], T.WB[:].indirect(T.ol[:, 128:256]), T.D[:], F.Silu)
-    s_a = V([v_wa, r_o, d_d], "cp", T.WA[:].indirect(T.ol[:, 0:128]), T.D[:])
+    s_b = ACT([a_wb, v_wb, p_z2, r_o, d_d], T.WB[:].indirect(T.ol[:, 128:256]), T.D[:], F.Silu)
+    s_a = V([v_wa, r_o, d_d, p_z], "cp", T.WA[:].indirect(T.ol[:, 0:128]), T.D[:])
 
-    BI, B8 = (T.BZ, 0), (T.BZ, 144)
-    ID = T.BZ[:, 288:416]
-    B2 = T.BZ[:, 416:424]
-    E = (T.BO, 0)
-    LS = T.BO[:, 144:272]
-    SG = T.BO[:, 272:400]
+    BI, B8, E = ((T.BZ, 144 * k) for k in range(3))
+    ID = T.BZ[:, 872:1000]
+    B2 = T.BZ[:, 432:448]
+    CH = T.BZ[:, 448:482]
+    ZG = [T.BZ[:, 488:616], T.BZ[:, 616:744], T.BZ[:, 743:872], T.R[:, 4111:4240]]
 
-    m_b8 = SEL([p_z], T.BZ[:, 144:288], [[-1, 144]], A.not_equal, 0.0625, 15, 16)
-    m_bi = m_b2 = p_z
-    for k, w in ((0, 4.0), (8, 4.0), (1, -0.0625), (9, -0.0625)):
-        m_bi = SEL([m_bi], T.BZ[:, 0:144], [[-16, 9], [-256, 16]], A.not_equal, w, 3840 - k, 1)
-    for k in (2, 10):
-        m_b2 = SEL([m_b2], B2, [[-16, 8]], A.not_equal, -0.0625, -k, 1)
-    IOTA([], T.R[:, 4096:4112], [[0, 16]], 0, 0)
-    v_zx = IOTA([], T.zx[:], [[0, 32]], 0, 0)
-    m_id = SEL([p_z], ID, [[-1, 128]], A.not_equal, 1.0, 0, 1)
-    IOTA([], T.BO[:, 128:144], [[0, 16]], 0, 0)
-    p_one = IOTA([], SG, [[0, 128]], 1, 0)
-    m = SEL([p_one], SG, [[-16, 8], [0, 16]], A.is_ge, 0.0, 0, 1)
-    m_sg = SEL([m], SG, [[16, 8], [0, 16]], A.is_ge, 0.0, 15, -1)
-    m_e = SELO([m_sg], T.BO[:, 0:128], SG, [[0, 8], [1, 16]], A.is_equal, -15, 0)
-    m_ls = SELO([m_sg], LS, SG, [[1, 128]], A.is_gt, 0, -1)
+    def last(mat):
+        return T.BZ[:, mat[1] + 15:mat[1] + 128:16]
+
+    m = IOTA([], T.Q[0:16], [[0, 68]], 0, 0)
+    p_r0 = IOTA([], T.R[:, 4096:4112], [[0, 16]], 0, 0)
+    IOTA([], T.K[:], [[4097, 2], [4095, 2]], -4096, 0)
+    IOTA([], T.K2[:], [[-1, 2], [1, 2]], 0, 0)
+    c_k = IOTA([], T.e1[:, 16:17], [[0, 1]], 4327, -1)
+    p_one = IOTA([], T.msk[:, 0:256], [[0, 256]], 1, 0)
+    r_n = SEND([v_nls], prv, T.nl[:], T.nls[:], "rn")
+    SEL([m], T.Q[0:16, 0, :], [[-1, 17]], A.is_ge, 1.0 / 4096, 0, 1)
+    SEL([], T.Q[0:16, 1, :], [[-1, 17]], A.not_equal, -1.0, 0, 1)
+    SEL([], T.Q[0:16, 2, :], [[1, 17]], A.is_gt, 1.0 / 4096, 0, -1)
+    m_q = SEL([], T.Q[0:16, 3, :], [[-1, 17]], A.not_equal, 1.0, 0, 1)
+    m_b8 = SEL([p_z], last(B8), [[-1, 8]], A.not_equal, 0.0625, 0, 1)
+    m_bi = m_b2 = m_b3 = m_b8
+    m = IOTA([], last(E), [[0, 8]], 1, 0)
+    for k in (0, 8):
+        m_bi = SEL([m_bi], last(BI), [[-16, 8]], A.not_equal, 4.0, -k, 1)
+        m_b2 = SEL([m_b2], B2[:, 0:8], [[-16, 8]], A.not_equal, -0.0625, -k - 2, 1)
+        m_bi = SEL([m_bi], last(BI), [[-16, 8]], A.not_equal, -0.0625, -k - 1, 1)
+        m = SEL([m], last(E), *(([[16, 8]], A.is_ge, 0.0, 15, -1) if k else ([[-16, 8]], A.is_ge, 0.0, 0, 1)))
+    SELO([p_one], ID, T.msk[:, 0:128], [[-1, 128]], A.is_equal, 0, 1)
+    for p in range(2):
+        m_b3 = SEL([m_b3], B2[:, 8:16], [[-16, 8]], A.not_equal, 16.0, -8 * p, 1)
+        m = SELO([], T.PM[:, 256 * p:256 * p + 256], T.msk[:, 0:256], [[-1, 16], [16, 16]], A.is_equal, 128 * p - 240, 1)
+    m_b3 = SEL([m_b3], B2[:, 8:16], [[-16, 8]], A.not_equal, -16.0, -4, 1)
+    m1 = SELO([], T.msk[:, 256:384], T.msk[:, 0:128], [[0, 8], [-16, 16]], A.is_ge, 111, -1)
+    SEL([m_b3], B2[:, 8:16], [[-16, 8]], A.not_equal, -16.0, -12, 1)
+    SEL([m], T.msk[:, 128:256], [[0, 8], [-16, 16]], A.is_ge, 0.0, 239, -1)
+    SEL([m1], T.msk[:, 0:128], [[0, 8], [1, 16]], A.not_equal, 0.0, 0, 0)
+
+    def late():
+        IOTA([], T.c2[:], [[30720, 2], [0, 32]], 0, 0)
+        IOTA([], CH[:, 17:34], [[0, 17]], 3072, -16)
+        IOTA([], T.lo[:], [[1, 17]], 0, 0)
+        return IOTA([], T.cv[:], [[1, 17], [-16, 16]], 240, 0)
 
     MM([m_b8, d_prow], rewrap(T.b7[:, 0:128], B8, T.prow, 0, 128, 8, False)
        + rewrap(T.b5[:, 0:128], B8, T.prow, 128, 256, 8, False), False)
 
-    def tlist(out, src, c0, c1):
-        return [(out[0:c1 - c0, t:128:16], src[:, 16 * c0 + t:16 * c1:16], B2, True, True) for t in range(16)]
+    def tlist(out, src, c0, c1, n=8):
+        return [(out[0:c1 - c0, t:16 * n:16], src[:, 16 * c0 + t:16 * c1:16], B2[:, 0:n], True, True) for t in range(16)]
 
-    IOTA([], T.K[:], [[4095, 2], [-4097, 2]], 1, 0)
-    IOTA([], T.K2[:], [[-4096, 2], [-4095, 2]], 4096, 0)
-    IOTA([], T.e1[:], [[1, 17]], 1025, 17)
-    IOTA([], T.pr[:], [[16, 16], [1, 18]], 0, 0, False)
-    IOTA([], T.cv[:], [[1, 272]], 0, 0)
+    DMA("s", "dk", [c_k], T.K[0::16, :], T.K2[0:8, :])
+    d_k = DMA("s", "dk", [], T.e1[0::16, 16:17], T.K2[0:8, 0:1])
+    for b in range(1, 8):
+        d_q = DMA("s", "dq", [m_q], T.Q[16 * b:16 * b + 16], T.Q[0:16])
 
     g_a = [ACT([s_b, r_n], el(T.bg, c0, c1), T.WB[:].indirect(T.nl[:, c0:c1]), F.Copy, None, -1.0) for c0, c1 in SUBS]
     upto = {}
     t_code = [None] * 4
     v_jl = [None] * 4
     r_x = [None] * 4
+    code = [T.b1[:, 0:64], T.b1[:, 64:128], T.b2[:, 0:64], T.b3[:, 0:64]]
 
     def jl(q):
-        cols = slice(64 * q, 64 * q + 64)
-        v_jl[q] = V([t_code[q]], "ts", T.jl[:, cols], T["b%d" % q][:, 0:64], 4096.0, None, A.add)
+        cols = slice(64 * q if q > 1 else 0, 64 * q + 64)
+        v_jl[q] = V([t_code[q]], "ts", T.jl[:, cols], code[q] if q > 1 else T.b1[:, 0:128], 4096.0, None, A.add)
         r_x[q] = SEND([v_jl[q]], nxc, T.jx[:, cols], T.jl[:, cols], "rx%d" % q)
 
     for k, (c0, c1) in enumerate(SUBS):
         upto[c1] = V([s_a, g_a[k], r_n], "tt", el(T.R, c0, c1), T.WA[:].indirect(T.nl[:, c0:c1]), el(T.bg, c0, c1), A.min)
         if c1 % 64 == 0:
             q = c1 // 64 - 1
-            t_code[q] = MM([upto[c1], m_bi], rewrap(T["b%d" % q][:, 0:64], BI, T.R, 64 * q, 64 * q + 64))
+            t_code[q] = MM([upto[c1], m_bi], rewrap(code[q], BI, T.R, 64 * q, 64 * q + 64))
             if q == 1:
-                MM([m_b2], tlist(T.b6[:, 0:128], T.R, 0, 128), False)
-        if c1 in (128, 192, 256):
+                t_p0 = MM([m_b2], tlist(T.b6[:, 0:128], T.R, 0, 128))
+        if c1 in (192, 256):
             jl(c1 // 64 - 2)
-        if c1 == 128:
-            c_late = IOTA([], T.d0[:], [[0, 512]], -1, 0)
-    DMA("s", "dk", [c_late], T.K[0::16, :], T.K2[0:8, :])
-    DMA("s", "dk", [], T.pri[:], T.pr[:])
-    DMA("s", "dk", [], T.e1[15::16, 16:17], T.K2[0:8, 2:3])
-    d_k = DMA("s", "dk", [], T.d0[0::16, :], T.zx[:])
-    DMA("s", "dwin", [d_k, g_a[-1]], T.WB[0::16, 4096:4097], T.K[1:9, 3:4])
-    DMA("s", "dwin", [], T.WB[1::16, 4096:4097], T.K2[0:8, 2:3])
+        if c1 == 192:
+            c_late = late()
+    ACT([t_p0], T.kfs[:, 0:128], T.b6[:, 0:128], F.Copy)
+    a_d0 = ACT([d_k, g_a[0]], T.d0[:], T.bg[:, 0:512], F.Identity, T.K[:, 0:1], 0.0)
+    DMA("s", "dwin", [d_k, g_a[-1]], T.WB[0::16, 4096:4097], T.K2[0:8, 2:3])
+    DMA("s", "dwin", [], T.WB[1::16, 4096:4097], T.K2[0:8, 0:1])
 
     def gx(c0, c1):
-        return el(T.R2, c0, c1), T.R[:].indirect(T.jx[:, c0:c1])
+        return el(T.R2, c0, c1), T.R[:, 0:4112].indirect(T.jx[:, c0:c1])
 
-    row = [upto[256], v_zx]
-    g1 = [ACT(row + [r_x[1]], *gx(64, 128), F.Copy), V(row + [r_x[0]], "cp", *gx(0, 44))]
+    row = [upto[256], p_r0]
+    g1 = [ACT(row + [r_x[1]], *gx(64, 128), F.Copy), V(row + [r_x[1]], "cp", *gx(0, 38))]
     jl(3)
-    g1.append(V([], "cp", *gx(44, 64)))
-    t_kf = MM([m_b2], tlist(T.b6[:, 128:256], T.R, 128, 256))
-    g2 = [V([r_x[2]], "cp", *gx(128, 164)), ACT([r_x[2]], *gx(164, 192), F.Copy)]
-    a_kf = ACT([t_kf], T.kfs[:], T.b6[:, 0:256], F.Copy)
+    g1.append(V([], "cp", *gx(38, 64)))
+    t_kf = MM([a_d0], tlist(T.b6[:, 128:256], T.R, 128, 256))
+    g2 = [V([r_x[2]], "cp", *gx(128, 160)), ACT([r_x[2]], *gx(160, 192), F.Copy)]
+    a_kf = ACT([t_kf], T.kfs[:, 128:256], T.b6[:, 128:256], F.Copy)
     r_f = SEND([a_kf], nxc, T.kfl[:], T.kfs[:], "rf")
-    t_k0 = MM(g1 + [v_jl[0]], tlist(T.b0, T.R2, 0, 128))
-
-    def back(bank, p):
-        return [(bank[:, 0:128], T.kX[:, 128 * p:128 * p + 128], ID, True, True)]
+    t_k0 = MM(g1 + [c_late], tlist(T.b0, T.R2, 0, 128, 16))
 
     def plus(bank, kt, last):
         return [(bank[:, 0:128], kt, ID, False, last)]
 
-    def kept(bank, p, tok):
-        return V([tok], "ts", T.kept[:, 128 * p:128 * p + 128], bank[:, 0:128], 0.5, None, A.is_gt)
+    def counts(p, bank, tok):
+        L, Z, G = T.L[:, 128 * p:128 * p + 128], ZG[p], ZG[2 + p]
+        vl = V([tok, c_late], "scan", L, bank[:, 127:255], T.msk[:, 0:128], 0.0, A.add, A.mult)
+        vz = V([vl], "tt", Z[:, 0:128:16], L[:, 15:128:16], bank[:, 143:256:16], A.add)
+        return vz, vl, V([vz], "scan", G[:, 1:129], Z[:, 0:128], T.msk[:, 128 * p + 128:128 * p + 256], 0.0, A.add, A.mult)
 
-    def zsum(s0, s1, first, last):
-        return [(T.b4[:, 0:16], moved(E, s), T.kept[:, 16 * s:16 * s + 16], first and s == s0, last and s == s1 - 1)
-                for s in range(s0, s1)]
+    def places(p):
+        Z, G = ZG[p], ZG[2 + p]
+        return [(T.b4[:, 0:34], Z[:, 0:128], T.Q[:, 0:2, :], False, False),
+                (T.b4[:, 0:34], G[:, 0:128], T.Q[:, 0:2, :], False, False),
+                (T.b4[:, 0:34], G[:, 1:129], T.Q[:, 2:4, :], False, p == 1)]
 
-    def column(bank, c0, n):
-        return [(bank[:, 0:n], moved(E, 0), T.cv[:, c0:c0 + n], True, False)]
+    def before(p):
+        return [(T.b2[:, 0:256], T.L[:, 128 * p:128 * p + 128], T.PM[:, 256 * p:256 * p + 256], False, p == 1)]
 
-    def before(bank, c0):
-        return [(bank[:, 0:128], LS, T.kept[:, c0:c0 + 128], False, True)]
-
-    a_k0 = ACT([t_k0], T.kX[:, 0:128], T.b0[:, 0:128], F.Copy)
-    g2.append(V([r_x[3]], "cp", *gx(192, 228)))
-    g2.append(ACT([r_x[3]], *gx(228, 256), F.Copy))
-    t_b0 = MM([a_k0, v_jl[2], m_id], back(T.b2, 0))
-    MM([a_kf, c_late, m_e], column(T.b0, 0, 128) + column(T.b6, 128, 144), False)
-    v_c0 = kept(T.b2, 0, t_b0)
-    t_k1 = MM(g2 + [v_jl[1]], tlist(T.b1, T.R2, 128, 256))
+    MM([c_late, v_jl[2], d_q], [(T.b4[:, 0:34], ID, CH, True, False), (T.b4[:, 17:34], ID, T.lo[:], False, False),
+                                (T.b2[:, 0:272], moved(E, 0), T.cv[:], True, False)], False)
+    g2.append(V([r_x[3]], "cp", *gx(192, 224)))
+    g2.append(ACT([r_x[3]], *gx(224, 256), F.Copy))
+    v_c0, _, v_g0 = counts(0, T.b0, t_k0)
+    t_k1 = MM(g2 + [v_jl[1]], tlist(T.b1, T.R2, 128, 256, 16))
+    a_k0 = ACT([v_c0], T.kX[:, 0:128], T.b0[:, 0:128], F.Copy)
+    MM([v_g0], before(0) + places(0), False)
     v_owf = V([l_own], "cp", T.owf[:], T.owi[:])
     DMA("s", "dwin", [v_owf], T.WB[0::16, 0:4096], T.owf[:])
-    v_perm = V([d_k], "cp", T.swp[:], T.pri[:])
-    V([], "ms", T.mk[:, 384:1024], 0.0)
-    ACT([], T.mk[:, 0:384], T.R[:, 0:384], F.Copy, None, 0.0)
-    a_k1 = ACT([t_k1], T.kX[:, 128:256], T.b1[:, 0:128], F.Copy)
-    MM([v_c0, m_e, m_ls], zsum(0, 4, True, False), False)
-    t_b1 = MM([a_k1, v_jl[3]], back(T.b3, 1))
-    t_l0 = MM([], before(T.b0, 0))
-    MM([], zsum(4, 8, False, False), False)
-    v_c1 = kept(T.b3, 1, t_b1)
-    ACT([t_l0], T.loc[:, 0:128], T.b0[:, 0:128], F.Copy)
-    t_l1 = MM([v_c1], before(T.b6, 128))
-    t_z = MM([], zsum(8, 16, False, True))
-    a_loc = ACT([t_l1], T.loc[:, 128:272], T.b6[:, 0:144], F.Copy)
-    a_dt = ACT([a_loc, v_perm], T.DT[:], T.loc[:].indirect(T.swp[:, 0:17]), F.Copy)
-    v_zc = V([t_z, d_k], "scan", T.zx[:, 1:17], T.R[:, 4096:4112], T.b4[:, 0:16], 0.0, A.add, A.add)
-    t_off = MM([v_zc], [(T.b1[:, 128:129], LS, T.zx[:, 16:17], True, True)])
-    t_y = MM([r_f], plus(T.b7, T.kfl[:, 0:128], False) + plus(T.b5, T.kfl[:, 128:256], False)
-             + plus(T.b7, T.kX[:, 0:128], True) + plus(T.b5, T.kX[:, 128:256], True))
-    ACT([t_y], T.YW[:, 0:128], T.b7[:, 0:128], F.Identity, -3.0)
-    a_yw = ACT([], T.YW[:, 128:256], T.b5[:, 0:128], F.Identity, -3.0)
+    ACT([], T.mk[:, 0:1024], T.R[:, 0:1024], F.Copy, None, 0.0)
+    v_c1, v_l1, v_g1 = counts(1, T.b1, t_k1)
+    a_k1 = ACT([v_c1], T.kX[:, 128:256], T.b1[:, 0:128], F.Copy)
+    t_l1 = MM([v_l1], before(1))
+    t_z = MM([v_g1], places(1))
+    t_y0 = MM([r_f, a_k0], plus(T.b7, T.kX[:, 0:128], False) + plus(T.b7, T.kfl[:, 0:128], True))
+    t_y1 = MM([a_k1], plus(T.b5, T.kfl[:, 128:256], False) + plus(T.b5, T.kX[:, 128:256], True))
+    a_dt = ACT([t_l1], T.DT[:], T.b2[:, 0:272], F.Copy)
+    ACT([t_y0], T.YW[:, 0:128], T.b7[:, 0:128], F.Identity, -3.0)
+    a_yw = ACT([t_y1], T.YW[:, 128:256], T.b5[:, 0:128], F.Identity, -3.0)
+    MM([], [(T.b0[:, 0:64], ID, T.c2[:], True, False), (T.b0[:, 0:64], ID, T.c2[:], False, False)], False)
     d_win = DMA("s", "dwin", [a_yw], T.WB[1::16, 0:4096], T.YW[:])
-    v_e0 = V([d_k], "ts", T.e0[:], T.b4[:, 0:16], 0.0, None, A.is_equal)
-    v_e1 = V([v_e0], "tt", T.e1[:, 0:16], T.e0[:], T.e1[:, 0:16], A.mult)
-    v_p1 = V([v_e1, v_zc], "tt", T.p1[:], T.e1[:], T.zx[:, 0:17], A.add)
-    v_zl = V([v_p1, t_off], "ts", T.zl[:, 0:17], T.p1[:], T.b1[:, 128:129], None, A.add)
+    v_e1 = V([t_z, d_k], "ts", T.e1[:, 0:16], T.b4[:, 17:33], 0.0, None, A.max)
+    v_p1 = V([v_e1], "tt", T.p1[:], T.e1[:], T.b4[:, 0:17], A.add)
+    v_zl = V([v_p1], "cp", T.zl[:, 0:17], T.p1[:])
     v_mks = V([v_zl, a_dt], "cp", T.mk[:].indirect(T.zl[:, 0:17]), T.DT[:])
-    v_s0 = V([v_mks], "scan", T.S[:, 0:512], T.d0[:], T.mk[:, 0:512], 0.0, A.add, A.max)
+    v_s0 = V([v_mks, a_d0], "scan", T.S[:, 0:512], T.d0[:], T.mk[:, 0:512], 0.0, A.add, A.max)
     v_s1 = V([v_s0], "scan", T.S[:, 512:1024], T.d0[:], T.mk[:, 512:1024], T.S[:, 511:512], A.add, A.max)
-    a_h = ACT([v_s0], T.hit[:, 0:512], T.S[:, 0:512], F.Relu, T.K[:, 2:3], T.K[:, 1:2])
-    v_h = V([v_s1], "ts", T.hit[:, 512:1024], T.S[:, 512:1024], T.K[:, 0:1], T.K[:, 1:2], A.min, A.mult)
-    t_h = MM([a_h, v_h], rewrap(T.b2[:, 0:64], E, T.hit, 0, 64))
-    v_o0 = V([t_h], "ts", T.off[:, 0:32], T.b2[:, 0:32], 0.0625, None, A.mult)
-    v_o1 = V([], "ts", T.off[:, 32:64], T.b2[:, 32:64], 0.0625, 3840.0, A.mult, A.add)
+    a_h = ACT([v_s0], T.hit[:, 0:512], T.S[:, 0:512], F.Relu, T.K[:, 3:4], T.K[:, 1:2])
+    v_h = V([v_s1], "ts", T.hit[:, 512:1024], T.S[:, 512:1024], 4096.0, T.K[:, 1:2], A.min, A.mult)
+    t_h = MM([a_h, v_h], [(T.b0[:, 0:64], moved(E, t), T.hit[:, t:1024:16], False, t == 15) for t in range(16)])
+    v_o = V([t_h], "ts", T.off[:], T.b0[:, 0:64], 0.0625, None, A.mult)
     win = T.WB[:, 0:4112]
-    a_r = ACT([v_o0, d_win], T.res[:, 0:512], win.indirect(T.off[:, 0:32]), F.Copy)
-    v_r = V([v_o1, d_win], "cp", T.res[:, 512:1024], win.indirect(T.off[:, 32:64]))
+    a_r = ACT([v_o, d_win], T.res[:, 0:512], win.indirect(T.off[:, 0:32]), F.Copy)
+    v_r = V([v_o, d_win], "cp", T.res[:, 512:1024], win.indirect(T.off[:, 32:64]))
     DMA("s", "dout", [a_r, v_r], T.yk[:], T.res[0::16, :])
     DMA("a", "dout", [a_r, v_r], T.ys[:], T.res[1::16, :])
     need("p", [(s, cnt[s]) for s in sorted(cnt)])

@@ -59,11 +59,11 @@ SCRATCH = {
 for _k in range(8):
     SCRATCH["b%d" % _k] = ("psum", [128, 512], "float32")
 SEMAPHORES = ["v", "a", "t", "p", "down", "dpts", "dnxt", "dd", "dz", "dprow", "dk", "dq", "dwin", "dout",
-              "rp", "ro", "rn", "rx1", "rx2", "rx3", "rf", "sent"]
+              "rp", "ro", "rn", "rx0", "rx1", "rx2", "rx3", "rf", "sent"]
 
 SUBS = [(k, k + 32) for k in range(0, 256, 32)]
-XZ, XA, XV, XP1, XP2 = 1024, 5600, 5908, 512, 192
-NV = 4
+XZ, XA, XD, XV, XP1 = 896, 4448, 5984, 6320, 512
+NV = 5
 
 
 def rank_program(g, core, T, topo):
@@ -164,7 +164,6 @@ def rank_program(g, core, T, topo):
 
     l_own = DMA("s", "down", [], T.owi[:], T.own[:])
     l_pts = DMA("s", "dpts", [], T.pti[:], T.pts[:])
-    l_nxt = DMA("s", "dnxt", [], T.nxi[:], T.nxt[:])
 
     c_pid = IOTA([], T.pid[:], [[1, 1]], 0, 1, False)
     c_j = IOTA([], T.jj[:], [[-4, 8]], 48, 0)
@@ -177,12 +176,13 @@ def rank_program(g, core, T, topo):
     v_sc = V([v_s, v_o1], "ts", T.sc[:], T.o1[:], 1.0, T.s16[:], A.is_equal, A.mult)
     V([], "ts", T.u4[:], T.o1[:], -4.0, T.s16[:], A.mult, A.add)
     v_ev = V([v_sc], "ts", T.ev[:], T.s16[:], T.sc[:], None, A.subtract)
+    V([], "ms", T.WA[:, 0:576], 0.0)
     v_ols = V([l_own], "cp", T.ols[:], T.owi[:])
     v_bias = V([v_ev, c_j], "ts", T.hb[:], T.jj[:], T.u4[:], T.ev[:], A.subtract, A.mult)
-    V([], "ms", T.WA[:, 0:384], 0.0)
+    v_wa0 = V([], "ms", T.WA[:, 576:1024], 0.0)
     v_pf = V([l_pts], "ts", T.pfs[:], T.pti[:], 1.0, T.s16[:], A.add, A.mult)
-    a5 = ACT([z0], T.WB[:, 64:128], T.WB[:, 0:64], F.Silu)
-    a5 = ACT([a5, z1], T.WB[:, XZ:2 * XZ], T.WB[:, 0:XZ], F.Silu)
+    a1 = ACT([z0], T.WB[:, 64:128], T.WB[:, 0:64], F.Silu)
+    a5 = ACT([a1, z1], T.WB[:, XZ:2 * XZ], T.WB[:, 0:XZ], F.Silu)
     for j in range(8):
         out = T.D[:, 256 * j:256 * j + 256]
         if j < NV:
@@ -191,24 +191,26 @@ def rank_program(g, core, T, topo):
             a_d = ACT([v_bias, c_x], out, T.xx[:], F.Identity, T.hb[:, j:j + 1], T.sc[:])
     for c in range(2 * XZ, XA, 2 * XZ):
         a_wb = ACT([a5], T.WB[:, c:min(c + 2 * XZ, XA)], T.WB[:, 0:min(2 * XZ, XA - c)], F.Silu)
-    v_wa0 = V([], "ms", T.WA[:, 384:768], 0.0)
     v_pb = V([], "ts", T.pb[:], T.pti[:], 16.0, 16.0, A.mult, A.add)
-    v_wb = V([], "ms", T.WB[:, XA:XV], 0.0)
-    v_nls = V([l_nxt], "cp", T.nls[:], T.nxi[:])
-    v_wa = V([], "ms", T.WA[:, 768:8192], 0.0)
+    v_wb = V([], "ms", T.WB[:, XD:XV], 0.0)
+    v_wa = V([], "ms", T.WA[:, 2048:8192], 0.0)
 
     def clear(c0, c1):
         return IOTA([], T.WB[:, c0:c1], [[0, c1 - c0]], 0, 0)
 
     clear(XV, XV + XP1)
     r_o = SEND([v_ols], opp, T.ol[:], T.ols[:], "ro", slice(1, None, 4))
-    clear(XV + XP1, XV + XP1 + XP2)
     r_p = SEND([v_pf], opp, T.pf[:], T.pfs[:], "rp", slice(0, None, 2))
-    p_z2 = clear(XV + XP1 + XP2, 8192)
+    p_z2 = clear(XV + XP1, 8192)
 
+    for c in range(XA, XD, XZ - 128):
+        DMA("s", "dd", [z1], T.WB[:, c:c + XZ - 128], T.WB[:, 128:XZ])
+    DMA("s", "dz", [v_wa0], T.WA[:, 1024:2048], T.WA[:, 0:1024])
     d_d = DMA("s", "dd", [r_p, a_d, v_d], T.D[2::8, :], T.pf[:])
+    l_nxt = DMA("s", "dnxt", [], T.nxi[:], T.nxt[:])
     p_z = DMA("s", "dz", [v_wa0], T.BZ[:, 0:744], T.WA[:, 0:744])
     d_prow = DMA("s", "dprow", [v_pb], T.prow[:], T.pb[:])
+    v_nls = V([l_nxt], "cp", T.nls[:], T.nxi[:])
 
     s_b = ACT([a_wb, v_wb, p_z2, r_o, d_d], T.WB[:].indirect(T.ol[:, 128:256]), T.D[:], F.Silu)
     s_a = V([v_wa, r_o, d_d, p_z], "cp", T.WA[:].indirect(T.ol[:, 0:128]), T.D[:])
@@ -249,13 +251,7 @@ def rank_program(g, core, T, topo):
     m1 = SELO([], T.msk[:, 256:384], T.msk[:, 0:128], [[0, 8], [-16, 16]], A.is_ge, 111, -1)
     SEL([m_b3], B2[:, 8:16], [[-16, 8]], A.not_equal, -16.0, -12, 1)
     SEL([m], T.msk[:, 128:256], [[0, 8], [-16, 16]], A.is_ge, 0.0, 239, -1)
-    SEL([m1], T.msk[:, 0:128], [[0, 8], [1, 16]], A.not_equal, 0.0, 0, 0)
-
-    def late():
-        IOTA([], T.c2[:], [[30720, 2], [0, 32]], 0, 0)
-        IOTA([], CH[:, 17:34], [[0, 17]], 3072, -16)
-        IOTA([], T.lo[:], [[1, 17]], 0, 0)
-        return IOTA([], T.cv[:], [[1, 17], [-16, 16]], 240, 0)
+    c_msk = SEL([m1], T.msk[:, 0:128], [[0, 8], [1, 16]], A.not_equal, 0.0, 0, 0)
 
     MM([m_b8, d_prow], rewrap(T.b7[:, 0:128], B8, T.prow, 0, 128, 8, False)
        + rewrap(T.b5[:, 0:128], B8, T.prow, 128, 256, 8, False), False)
@@ -273,11 +269,11 @@ def rank_program(g, core, T, topo):
     t_code = [None] * 4
     v_jl = [None] * 4
     r_x = [None] * 4
-    code = [T.b1[:, 0:64], T.b1[:, 64:128], T.b2[:, 0:64], T.b3[:, 0:64]]
+    code = [T["b%d" % q][:, 0:64] for q in range(4)]
 
     def jl(q):
-        cols = slice(64 * q if q > 1 else 0, 64 * q + 64)
-        v_jl[q] = V([t_code[q]], "ts", T.jl[:, cols], code[q] if q > 1 else T.b1[:, 0:128], 4096.0, None, A.add)
+        cols = slice(64 * q, 64 * q + 64)
+        v_jl[q] = V([t_code[q]], "ts", T.jl[:, cols], code[q], 4096.0, None, A.add)
         r_x[q] = SEND([v_jl[q]], nxc, T.jx[:, cols], T.jl[:, cols], "rx%d" % q)
 
     for k, (c0, c1) in enumerate(SUBS):
@@ -287,11 +283,9 @@ def rank_program(g, core, T, topo):
             t_code[q] = MM([upto[c1], m_bi], rewrap(code[q], BI, T.R, 64 * q, 64 * q + 64))
             if q == 1:
                 t_p0 = MM([m_b2], tlist(T.b6[:, 0:128], T.R, 0, 128))
-        if c1 in (192, 256):
+        if c1 in (128, 192, 256):
             jl(c1 // 64 - 2)
-        if c1 == 192:
-            c_late = late()
-    ACT([t_p0], T.kfs[:, 0:128], T.b6[:, 0:128], F.Copy)
+    a_f0 = ACT([t_p0], T.kfs[:, 0:128], T.b6[:, 0:128], F.Copy)
     a_d0 = ACT([d_k, g_a[0]], T.d0[:], T.bg[:, 0:512], F.Identity, T.K[:, 0:1], 0.0)
     DMA("s", "dwin", [d_k, g_a[-1]], T.WB[0::16, 4096:4097], T.K2[0:8, 2:3])
     DMA("s", "dwin", [], T.WB[1::16, 4096:4097], T.K2[0:8, 0:1])
@@ -300,21 +294,25 @@ def rank_program(g, core, T, topo):
         return el(T.R2, c0, c1), T.R[:, 0:4112].indirect(T.jx[:, c0:c1])
 
     row = [upto[256], p_r0]
-    g1 = [ACT(row + [r_x[1]], *gx(64, 128), F.Copy), V(row + [r_x[1]], "cp", *gx(0, 38))]
+    g1 = [ACT(row + [r_x[0]], *gx(36, 64), F.Copy), V(row + [r_x[0]], "cp", *gx(0, 36))]
     jl(3)
-    g1.append(V([], "cp", *gx(38, 64)))
-    t_kf = MM([a_d0], tlist(T.b6[:, 128:256], T.R, 128, 256))
+    IOTA([], CH[:, 17:34], [[0, 17]], 3072, -16)
+    IOTA([], T.lo[:], [[1, 17]], 0, 0)
+    c_late = IOTA([], T.cv[:], [[1, 17], [-16, 16]], 240, 0)
+    g1 += [ACT([r_x[1]], *gx(92, 128), F.Copy), V([r_x[1]], "cp", *gx(64, 92))]
+    t_kf = MM([a_f0], tlist(T.b6[:, 128:256], T.R, 128, 256))
     g2 = [V([r_x[2]], "cp", *gx(128, 160)), ACT([r_x[2]], *gx(160, 192), F.Copy)]
     a_kf = ACT([t_kf], T.kfs[:, 128:256], T.b6[:, 128:256], F.Copy)
     r_f = SEND([a_kf], nxc, T.kfl[:], T.kfs[:], "rf")
-    t_k0 = MM(g1 + [c_late], tlist(T.b0, T.R2, 0, 128, 16))
+    c_c2 = IOTA([], T.c2[:], [[30720, 2], [0, 32]], 0, 0)
+    t_k0 = MM(g1 + [c_msk], tlist(T.b0, T.R2, 0, 128, 16))
 
     def plus(bank, kt, last):
         return [(bank[:, 0:128], kt, ID, False, last)]
 
     def counts(p, bank, tok):
         L, Z, G = T.L[:, 128 * p:128 * p + 128], ZG[p], ZG[2 + p]
-        vl = V([tok, c_late], "scan", L, bank[:, 127:255], T.msk[:, 0:128], 0.0, A.add, A.mult)
+        vl = V([tok, c_msk], "scan", L, bank[:, 127:255], T.msk[:, 0:128], 0.0, A.add, A.mult)
         vz = V([vl], "tt", Z[:, 0:128:16], L[:, 15:128:16], bank[:, 143:256:16], A.add)
         return vz, vl, V([vz], "scan", G[:, 1:129], Z[:, 0:128], T.msk[:, 128 * p + 128:128 * p + 256], 0.0, A.add, A.mult)
 
@@ -347,7 +345,7 @@ def rank_program(g, core, T, topo):
     a_dt = ACT([t_l1], T.DT[:], T.b2[:, 0:272], F.Copy)
     ACT([t_y0], T.YW[:, 0:128], T.b7[:, 0:128], F.Identity, -3.0)
     a_yw = ACT([t_y1], T.YW[:, 128:256], T.b5[:, 0:128], F.Identity, -3.0)
-    MM([], [(T.b0[:, 0:64], ID, T.c2[:], True, False), (T.b0[:, 0:64], ID, T.c2[:], False, False)], False)
+    MM([c_c2], [(T.b0[:, 0:64], ID, T.c2[:], True, False), (T.b0[:, 0:64], ID, T.c2[:], False, False)], False)
     d_win = DMA("s", "dwin", [a_yw], T.WB[1::16, 0:4096], T.YW[:])
     v_e1 = V([t_z, d_k], "ts", T.e1[:, 0:16], T.b4[:, 17:33], 0.0, None, A.max)
     v_p1 = V([v_e1], "tt", T.p1[:], T.e1[:], T.b4[:, 0:17], A.add)

@@ -17,7 +17,7 @@ SCRATCH = {
     "WA": ("sbuf", [128, 8192], "bfloat16"),
     "WB": ("sbuf", [128, 8192], "float32"),
     "bg": ("sbuf", [128, 4096], "bfloat16"),
-    "R": ("sbuf", [128, 4240], "bfloat16"),
+    "R": ("sbuf", [128, 4112], "bfloat16"),
     "R2": ("sbuf", [128, 4096], "bfloat16"),
     "prow": ("sbuf", [8, 4096], "bfloat16"),
     "pid": ("sbuf", [128, 1], "int32"),
@@ -30,40 +30,42 @@ SCRATCH = {
     "jj": ("sbuf", [128, 8], "float32"),
     "hb": ("sbuf", [128, 8], "float32"),
     "xx": ("sbuf", [128, 256], "float32"),
-    "K": ("sbuf", [128, 4], "float32"),
+    "K": ("sbuf", [128, 1], "float32"),
     "K2": ("sbuf", [128, 4], "float32"),
-    "BZ": ("sbuf", [128, 1000], "bfloat16"),
-    "Q": ("sbuf", [128, 4, 17], "bfloat16"),
-    "lo": ("sbuf", [128, 17], "bfloat16"),
-    "c2": ("sbuf", [128, 64], "bfloat16"),
-    "msk": ("sbuf", [128, 384], "bfloat16"),
-    "PM": ("sbuf", [128, 512], "bfloat16"),
+    "BZ": ("sbuf", [128, 1208], "bfloat16"),
+    "Q": ("sbuf", [128, 80], "bfloat16"),
+    "lo": ("sbuf", [128, 18], "bfloat16"),
+    "one": ("sbuf", [128, 144], "bfloat16"),
+    "msk": ("sbuf", [128, 400], "bfloat16"),
+    "PM": ("sbuf", [128, 144], "bfloat16"),
+    "H": ("sbuf", [128, 128], "bfloat16"),
     "L": ("sbuf", [128, 256], "bfloat16"),
-    "cv": ("sbuf", [128, 272], "bfloat16"),
-    "d0": ("sbuf", [128, 512], "bfloat16"),
-    "mk": ("sbuf", [128, 5376], "bfloat16"),
+    "cv": ("sbuf", [33, 144], "bfloat16"),
+    "d0": ("sbuf", [128, 1024], "bfloat16"),
+    "mk": ("sbuf", [128, 7520], "bfloat16"),
     "S": ("sbuf", [128, 1024], "bfloat16"),
-    "hit": ("sbuf", [128, 1024], "bfloat16"),
     "off": ("sbuf", [128, 64], "uint16"),
     "kX": ("sbuf", [128, 256], "bfloat16"),
     "kfs": ("sbuf", [128, 256], "bfloat16"),
     "kfl": ("sbuf", [128, 256], "bfloat16"),
-    "DT": ("sbuf", [128, 272], "bfloat16"),
-    "e1": ("sbuf", [128, 17], "float32"),
-    "p1": ("sbuf", [128, 17], "float32"),
-    "zl": ("sbuf", [128, 18], "uint16"),
+    "DT": ("sbuf", [128, 288], "bfloat16"),
+    "p1": ("sbuf", [128, 18], "float32"),
+    "zl": ("sbuf", [128, 20], "uint16"),
     "YW": ("sbuf", [128, 256], "float32"),
     "owf": ("sbuf", [128, 256], "float32"),
     "res": ("sbuf", [128, 1024], "float32"),
 }
 for _k in range(8):
     SCRATCH["b%d" % _k] = ("psum", [128, 512], "float32")
-SEMAPHORES = ["v", "a", "t", "p", "down", "dpts", "dnxt", "dd", "dz", "dprow", "dk", "dq", "dwin", "dout",
+SEMAPHORES = ["v", "a", "t", "p", "down", "dpts", "dnxt", "dd", "dz", "dprow", "dk", "dq", "dw", "dy", "dm", "dg", "dwin", "dout",
               "rp", "ro", "rn", "rx0", "rx1", "rx2", "rx3", "rf", "sent"]
 
 SUBS = [(k, k + 32) for k in range(0, 256, 32)]
-XZ, XA, XD, XV, XP1 = 896, 4448, 5984, 6320, 512
+XZ, XA, XD, XV, XP1 = 896, 4384, 5920, 6360, 512
+W0, PRE = 576, 0
 NV = 5
+G2 = (38, 24, 48, 10)
+GROW, CAP = 2.0 ** 14, 2.0 ** 99
 
 
 def rank_program(g, core, T, topo):
@@ -122,13 +124,9 @@ def rank_program(g, core, T, topo):
         ins = g.iota(out, pattern, base, cm, allow_small_or_imprecise_dtypes=True) if small else g.iota(out, pattern, base, cm)
         return done("p", ins, 1)
 
-    def SEL(toks, buf, pattern, cmp, fill, base, cm):
+    def SEL(toks, buf, pattern, cmp, fill, base, cm, src=None):
         need("p", toks)
-        return done("p", g.affine_select(buf, buf, pattern, cmp, fill, base, cm), 1)
-
-    def SELO(toks, out, src, pattern, cmp, base, cm):
-        need("p", toks)
-        return done("p", g.affine_select(out, src, pattern, cmp, 0.0, base, cm), 1)
+        return done("p", g.affine_select(buf, buf if src is None else src, pattern, cmp, fill, base, cm), 1)
 
     def DMA(q, s, toks, out, in_):
         need(q, toks)
@@ -156,8 +154,8 @@ def rank_program(g, core, T, topo):
         buf, c = mat
         return buf[0:K, c + 15 - t:c + 143 - t]
 
-    def rewrap(out, mat, src, c0, c1, K=128, close=True):
-        return [(out, moved(mat, t, K), src[0:K, 16 * c0 + t:16 * c1:16], t == 0, close and t == 15) for t in range(16)]
+    def rewrap(out, mat, src, c0, c1, K=128, alone=True):
+        return [(out, moved(mat, t, K), src[0:K, 16 * c0 + t:16 * c1:16], alone and t == 0, alone and t == 15) for t in range(16)]
 
     def el(buf, c0, c1):
         return buf[:, 16 * c0:16 * c1]
@@ -174,12 +172,12 @@ def rank_program(g, core, T, topo):
     v_o1 = V([], "ts", T.o1[:], T.pid[:], 5, None, A.bitwise_and)
     v_s = V([v_h8], "ts", T.s16[:], T.h8[:], 4.0, -16.0, A.mult, A.add)
     v_sc = V([v_s, v_o1], "ts", T.sc[:], T.o1[:], 1.0, T.s16[:], A.is_equal, A.mult)
-    V([], "ts", T.u4[:], T.o1[:], -4.0, T.s16[:], A.mult, A.add)
+    V([], "ts", T.u4[:], T.o1[:], -127.0, T.s16[:], A.mult, A.add)
     v_ev = V([v_sc], "ts", T.ev[:], T.s16[:], T.sc[:], None, A.subtract)
-    V([], "ms", T.WA[:, 0:576], 0.0)
+    V([], "ms", T.WA[:, 0:W0], 0.0)
     v_ols = V([l_own], "cp", T.ols[:], T.owi[:])
     v_bias = V([v_ev, c_j], "ts", T.hb[:], T.jj[:], T.u4[:], T.ev[:], A.subtract, A.mult)
-    v_wa0 = V([], "ms", T.WA[:, 576:1024], 0.0)
+    v_wa0 = V([], "ms", T.WA[:, W0:1024], 0.0)
     v_pf = V([l_pts], "ts", T.pfs[:], T.pti[:], 1.0, T.s16[:], A.add, A.mult)
     a1 = ACT([z0], T.WB[:, 64:128], T.WB[:, 0:64], F.Silu)
     a5 = ACT([a1, z1], T.WB[:, XZ:2 * XZ], T.WB[:, 0:XZ], F.Silu)
@@ -191,7 +189,6 @@ def rank_program(g, core, T, topo):
             a_d = ACT([v_bias, c_x], out, T.xx[:], F.Identity, T.hb[:, j:j + 1], T.sc[:])
     for c in range(2 * XZ, XA, 2 * XZ):
         a_wb = ACT([a5], T.WB[:, c:min(c + 2 * XZ, XA)], T.WB[:, 0:min(2 * XZ, XA - c)], F.Silu)
-    v_pb = V([], "ts", T.pb[:], T.pti[:], 16.0, 16.0, A.mult, A.add)
     v_wb = V([], "ms", T.WB[:, XD:XV], 0.0)
     v_wa = V([], "ms", T.WA[:, 2048:8192], 0.0)
 
@@ -208,155 +205,194 @@ def rank_program(g, core, T, topo):
     DMA("s", "dz", [v_wa0], T.WA[:, 1024:2048], T.WA[:, 0:1024])
     d_d = DMA("s", "dd", [r_p, a_d, v_d], T.D[2::8, :], T.pf[:])
     l_nxt = DMA("s", "dnxt", [], T.nxi[:], T.nxt[:])
-    p_z = DMA("s", "dz", [v_wa0], T.BZ[:, 0:744], T.WA[:, 0:744])
-    d_prow = DMA("s", "dprow", [v_pb], T.prow[:], T.pb[:])
+    p_z = DMA("s", "dz", [v_wa0], T.BZ[:, 0:496], T.WA[:, 0:496])
     v_nls = V([l_nxt], "cp", T.nls[:], T.nxi[:])
 
     s_b = ACT([a_wb, v_wb, p_z2, r_o, d_d], T.WB[:].indirect(T.ol[:, 128:256]), T.D[:], F.Silu)
     s_a = V([v_wa, r_o, d_d, p_z], "cp", T.WA[:].indirect(T.ol[:, 0:128]), T.D[:])
 
-    BI, B8, E = ((T.BZ, 144 * k) for k in range(3))
-    ID = T.BZ[:, 872:1000]
-    B2 = T.BZ[:, 432:448]
-    CH = T.BZ[:, 448:482]
-    ZG = [T.BZ[:, 488:616], T.BZ[:, 616:744], T.BZ[:, 743:872], T.R[:, 4111:4240]]
+    BY, CH, G, O = T.BZ[0:8, 0:16], T.BZ[:, 16:34], T.BZ[:, 39:168], T.BZ[:, 168:311]
+    BI, E = (T.BZ, 296), (T.BZ, 424)
+    B2 = T.BZ[:, 567:936:16]
+    ALL = T.BZ[:, 311:936:16]
+    RT = T.BZ[:, 952:1080]
+    ID = T.BZ[:, 1080:1208]
+    NIL, ONE = T.BZ[0:1, 40:168], T.one[0:1, 0:128]
+    DMA("s", "dy", [p_z], T.BZ[:, 496:952], T.BZ[:, 40:496])
+    p_y = DMA("s", "dy", [], T.R[:, 4096:4112], T.BZ[:, 40:56])
 
-    def last(mat):
-        return T.BZ[:, mat[1] + 15:mat[1] + 128:16]
+    def repeat(sem, tok, cols, k):
+        for n in (k, 4 * k):
+            for b in (n, 2 * n, 3 * n):
+                e = min(b + n, 128)
+                d = DMA("s", sem, [tok], T.Q[b:e, cols], T.Q[0:e - b, cols])
+            tok = d
+        return tok
 
-    m = IOTA([], T.Q[0:16], [[0, 68]], 0, 0)
-    p_r0 = IOTA([], T.R[:, 4096:4112], [[0, 16]], 0, 0)
-    IOTA([], T.K[:], [[4097, 2], [4095, 2]], -4096, 0)
-    IOTA([], T.K2[:], [[-1, 2], [1, 2]], 0, 0)
-    c_k = IOTA([], T.e1[:, 16:17], [[0, 1]], 4327, -1)
-    p_one = IOTA([], T.msk[:, 0:256], [[0, 256]], 1, 0)
+    m_pb = SEL([v_pf], T.pb[:], [[0, 256]], A.is_equal, 0.0, 0, 0, T.pfs[:])
+    m = IOTA([], T.Q[0:9, :], [[0, 80]], 0, 0)
+    IOTA([], T.K[:], [[0, 1]], int(GROW), 0)
+    IOTA([m], T.Q[0:8, 48:56], [[0, 8]], 1, 0)
+    m0 = SEL([], T.Q[0:8, 40:48], [[0, 8]], A.not_equal, 4.0, 0, 1)
+    m1 = SEL([], T.Q[0:8, 56:72], [[0, 16]], A.not_equal, -129.0 / 2 ** 20, 0, 1)
+    SEL([], T.Q[0:8, 72:80], [[0, 8]], A.not_equal, -0.0625, -2, 1)
+    SEL([m0], T.Q[0:8, 40:48], [[0, 8]], A.not_equal, -0.0625, -1, 1)
+    m_w = SEL([m1], T.Q[0:8, 56:72], [[0, 16]], A.not_equal, 129.0 / 2 ** 20, -4, 1)
     r_n = SEND([v_nls], prv, T.nl[:], T.nls[:], "rn")
-    SEL([m], T.Q[0:16, 0, :], [[-1, 17]], A.is_ge, 1.0 / 4096, 0, 1)
-    SEL([], T.Q[0:16, 1, :], [[-1, 17]], A.not_equal, -1.0, 0, 1)
-    SEL([], T.Q[0:16, 2, :], [[1, 17]], A.is_gt, 1.0 / 4096, 0, -1)
-    m_q = SEL([], T.Q[0:16, 3, :], [[-1, 17]], A.not_equal, 1.0, 0, 1)
-    m_b8 = SEL([p_z], last(B8), [[-1, 8]], A.not_equal, 0.0625, 0, 1)
-    m_bi = m_b2 = m_b3 = m_b8
-    m = IOTA([], last(E), [[0, 8]], 1, 0)
-    for k in (0, 8):
-        m_bi = SEL([m_bi], last(BI), [[-16, 8]], A.not_equal, 4.0, -k, 1)
-        m_b2 = SEL([m_b2], B2[:, 0:8], [[-16, 8]], A.not_equal, -0.0625, -k - 2, 1)
-        m_bi = SEL([m_bi], last(BI), [[-16, 8]], A.not_equal, -0.0625, -k - 1, 1)
-        m = SEL([m], last(E), *(([[16, 8]], A.is_ge, 0.0, 15, -1) if k else ([[-16, 8]], A.is_ge, 0.0, 0, 1)))
-    SELO([p_one], ID, T.msk[:, 0:128], [[-1, 128]], A.is_equal, 0, 1)
-    for p in range(2):
-        m_b3 = SEL([m_b3], B2[:, 8:16], [[-16, 8]], A.not_equal, 16.0, -8 * p, 1)
-        m = SELO([], T.PM[:, 256 * p:256 * p + 256], T.msk[:, 0:256], [[-1, 16], [16, 16]], A.is_equal, 128 * p - 240, 1)
-    m_b3 = SEL([m_b3], B2[:, 8:16], [[-16, 8]], A.not_equal, -16.0, -4, 1)
-    m1 = SELO([], T.msk[:, 256:384], T.msk[:, 0:128], [[0, 8], [-16, 16]], A.is_ge, 111, -1)
-    SEL([m_b3], B2[:, 8:16], [[-16, 8]], A.not_equal, -16.0, -12, 1)
-    SEL([m], T.msk[:, 128:256], [[0, 8], [-16, 16]], A.is_ge, 0.0, 239, -1)
-    c_msk = SEL([m1], T.msk[:, 0:128], [[0, 8], [1, 16]], A.not_equal, 0.0, 0, 0)
+    d_prow = DMA("s", "dprow", [m_pb], T.prow[:], T.pb[:])
+    d_w = repeat("dw", m_w, slice(40, 80), 8)
+    SEL([p_z], BY[:, 0:8], [[-1, 8]], A.not_equal, -0.0625, 0, 1)
+    m_by = SEL([], BY[:, 8:16], [[-1, 8]], A.not_equal, 0.0625, 0, 1)
+    c_k = IOTA([], T.K2[:], [[-1, 2], [1, 2]], 0, 0)
+    p_one = IOTA([], T.one[:], [[0, 144]], 1, 0)
+    m_mk = SEL([p_one], T.mk[:, 0:128], [[0, 128]], A.not_equal, CAP, 0, 0, T.one[:, 0:128])
+    SEL([p_y], ID, [[-1, 128]], A.is_equal, 0.0, 0, 1, T.one[:, 0:128])
+    SEL([m_mk], RT, [[0, 8], [1, 16]], A.is_equal, 0.0, 0, 0, T.mk[:, 0:128])
+    m = SEL([d_w], ALL, [[0, 5], [-16, 8]], A.is_ge, 0.0, 0, 1, T.Q[:, 40:80])
+    IOTA([], CH[:, 1:18:2], [[0, 9]], 6144, -32)
+    m_bi = SEL([m], ALL, [[0, 5], [16, 8]], A.is_ge, 0.0, 15, -1)
+    IOTA([], T.lo[:], [[432, 2], [-2, 9]], 0, 0)
+    SEL([m_bi], ALL[:, 8:16], [[-16, 8]], A.not_equal, -1.0 / 256, 0, 1)
+    c_cv = IOTA([], T.cv[:], [[-1, 9], [9, 16]], -136, -4)
 
-    MM([m_b8, d_prow], rewrap(T.b7[:, 0:128], B8, T.prow, 0, 128, 8, False)
-       + rewrap(T.b5[:, 0:128], B8, T.prow, 128, 256, 8, False), False)
+    def tlist(out, src, c0, mat, n, start, stop, K=128):
+        return [(out[:, t:16 * n:16], src[0:K, 16 * c0 + t:16 * c0 + 2048:16], mat, start, start or (stop and t == 15))
+                for t in range(16)]
 
-    def tlist(out, src, c0, c1, n=8):
-        return [(out[0:c1 - c0, t:16 * n:16], src[:, 16 * c0 + t:16 * c1:16], B2[:, 0:n], True, True) for t in range(16)]
+    for p, bank in enumerate((T.b0, T.b1)):
+        MM([m_by, d_prow], [(bank[:, 0:384], NIL, T.prow[0:1, 0:384], True, False)]
+           + tlist(bank[:, 256:384], T.prow, 128 * p, BY[:, 8 * p:8 * p + 8], 8, False, False, 8), False)
+    MM([p_one], [(bank[:, 128:256], ONE, ONE, False, False) for bank in (T.b0, T.b1)], False)
 
-    DMA("s", "dk", [c_k], T.K[0::16, :], T.K2[0:8, :])
-    d_k = DMA("s", "dk", [], T.e1[0::16, 16:17], T.K2[0:8, 0:1])
-    for b in range(1, 8):
-        d_q = DMA("s", "dq", [m_q], T.Q[16 * b:16 * b + 16], T.Q[0:16])
+    d_k = DMA("s", "dk", [c_k], T.K[0::16, :], T.K2[0:8, 1:2])
+    d_m = m_mk
+    for b in (128, 256, 512):
+        d_m = DMA("s", "dm", [d_m], T.mk[:, b:2 * b], T.mk[:, 0:b])
+
+    def columns(p, bank):
+        jobs = [(bank[:, 0:144], RT[32 * p:32 * p + 1, :], T.cv[32 * p:32 * p + 1, :], True, False)]
+        return jobs + [(bank[:, 0:1], lhs[32:33, 0:128], T.one[32:33, 0:1], False, False) for lhs in (T.mk, RT)] * p
+
+    def spare(p, bank):
+        return [(bank[:, 0:18], ID, CH, True, False), (bank[:, 1:18:2], ID, T.lo[:, 0:9], False, False),
+                (bank[:, 2 * p:18:2], moved(E, 0), T.lo[:, 9 + p:18], False, False),
+                (bank[:, 1:18:2], RT[0:1, :], T.cv[0:1, 0:9], False, False)]
 
     g_a = [ACT([s_b, r_n], el(T.bg, c0, c1), T.WB[:].indirect(T.nl[:, c0:c1]), F.Copy, None, -1.0) for c0, c1 in SUBS]
     upto = {}
     t_code = [None] * 4
     v_jl = [None] * 4
     r_x = [None] * 4
-    code = [T["b%d" % q][:, 0:64] for q in range(4)]
+    code = [T["b%d" % (2 + q % 2)][:, 0:64] for q in range(4)]
+    late = {}
 
     def jl(q):
         cols = slice(64 * q, 64 * q + 64)
         v_jl[q] = V([t_code[q]], "ts", T.jl[:, cols], code[q], 4096.0, None, A.add)
         r_x[q] = SEND([v_jl[q]], nxc, T.jx[:, cols], T.jl[:, cols], "rx%d" % q)
+        if q == 0:
+            SEL([], T.Q[0:9, 0:18:2], [[-1, 9]], A.is_ge, 1.0, 0, 1)
+            SEL([], T.Q[0:9, 1:18:2], [[-1, 9]], A.not_equal, -8192.0, 0, 1)
+            SEL([], T.Q[0:9, 18:36:2], [[1, 9]], A.is_gt, 1.0, 0, -1)
+            m_q = SEL([], T.Q[0:9, 19:36:2], [[-1, 9]], A.not_equal, 8192.0, 0, 1)
+            late["q"] = repeat("dq", m_q, slice(0, 40), 9)
+            SEL([], T.msk[:, 0:128], [[0, 8], [-9, 16]], A.is_ge, 0.0, 134, -1, T.one[:, 0:128])
+        if q == 1:
+            m = SEL([], T.msk[:, 128:272], [[0, 9], [1, 16]], A.not_equal, 0.0, 0, 0, T.one[:])
+            SEL([], T.PM[:], [[-1, 9], [9, 16]], A.is_equal, 0.0, -135, 1, T.one[:])
+            late["msk"] = SEL([m], T.msk[:, 272:400], [[0, 8], [1, 16]], A.not_equal, -1.0, -15, 0, T.msk[:, 128:256])
 
     for k, (c0, c1) in enumerate(SUBS):
         upto[c1] = V([s_a, g_a[k], r_n], "tt", el(T.R, c0, c1), T.WA[:].indirect(T.nl[:, c0:c1]), el(T.bg, c0, c1), A.min)
         if c1 % 64 == 0:
             q = c1 // 64 - 1
-            t_code[q] = MM([upto[c1], m_bi], rewrap(code[q], BI, T.R, 64 * q, 64 * q + 64))
+            t_code[q] = MM([upto[c1], m_bi] + ([v_jl[q - 2]] if q > 1 else []), rewrap(code[q], BI, T.R, 64 * q, 64 * q + 64))
             if q == 1:
-                t_p0 = MM([m_b2], tlist(T.b6[:, 0:128], T.R, 0, 128))
+                t_p0 = MM([], tlist(T.b6[:, 0:128], T.R, 0, B2[:, 16:24], 8, True, True))
+            if q == PRE:
+                MM([c_cv], spare(0, T.b4) + columns(0, T.b5) + spare(1, T.b7), False)
         if c1 in (128, 192, 256):
             jl(c1 // 64 - 2)
     a_f0 = ACT([t_p0], T.kfs[:, 0:128], T.b6[:, 0:128], F.Copy)
-    a_d0 = ACT([d_k, g_a[0]], T.d0[:], T.bg[:, 0:512], F.Identity, T.K[:, 0:1], 0.0)
-    DMA("s", "dwin", [d_k, g_a[-1]], T.WB[0::16, 4096:4097], T.K2[0:8, 2:3])
-    DMA("s", "dwin", [], T.WB[1::16, 4096:4097], T.K2[0:8, 0:1])
+    a_d0 = ACT([d_k, g_a[0]], T.d0[:, 0:512], T.bg[:, 0:512], F.Identity, T.K[:, 0:1], 0.0)
+    DMA("s", "dwin", [d_k, g_a[-1]], T.WB[0::16, 4102:4103], T.K2[0:8, 2:3])
+    DMA("s", "dwin", [], T.WB[1::16, 4102:4103], T.K2[0:8, 0:1])
+    d_g = DMA("s", "dg", [a_d0], T.d0[:, 512:1024], T.d0[:, 0:512])
 
-    def gx(c0, c1):
-        return el(T.R2, c0, c1), T.R[:, 0:4112].indirect(T.jx[:, c0:c1])
+    def gv(q, toks=()):
+        c0, c1 = 64 * q, 64 * q + G2[q]
+        return V(list(toks) + [r_x[q]], "cp", el(T.R2, c0, c1), T.R[:].indirect(T.jx[:, c0:c1]))
 
-    row = [upto[256], p_r0]
-    g1 = [ACT(row + [r_x[0]], *gx(36, 64), F.Copy), V(row + [r_x[0]], "cp", *gx(0, 36))]
-    jl(3)
-    IOTA([], CH[:, 17:34], [[0, 17]], 3072, -16)
-    IOTA([], T.lo[:], [[1, 17]], 0, 0)
-    c_late = IOTA([], T.cv[:], [[1, 17], [-16, 16]], 240, 0)
-    g1 += [ACT([r_x[1]], *gx(92, 128), F.Copy), V([r_x[1]], "cp", *gx(64, 92))]
-    t_kf = MM([a_f0], tlist(T.b6[:, 128:256], T.R, 128, 256))
-    g2 = [V([r_x[2]], "cp", *gx(128, 160)), ACT([r_x[2]], *gx(160, 192), F.Copy)]
-    a_kf = ACT([t_kf], T.kfs[:, 128:256], T.b6[:, 128:256], F.Copy)
-    r_f = SEND([a_kf], nxc, T.kfl[:], T.kfs[:], "rf")
-    c_c2 = IOTA([], T.c2[:], [[30720, 2], [0, 32]], 0, 0)
-    t_k0 = MM(g1 + [c_msk], tlist(T.b0, T.R2, 0, 128, 16))
-
-    def plus(bank, kt, last):
-        return [(bank[:, 0:128], kt, ID, False, last)]
+    def ga(q, toks=()):
+        c0, c1 = 64 * q + G2[q], 64 * q + 64
+        return ACT(list(toks) + [r_x[q]], el(T.R2, c0, c1), T.R[:].indirect(T.jx[:, c0:c1]), F.Copy)
 
     def counts(p, bank, tok):
-        L, Z, G = T.L[:, 128 * p:128 * p + 128], ZG[p], ZG[2 + p]
-        vl = V([tok, c_msk], "scan", L, bank[:, 127:255], T.msk[:, 0:128], 0.0, A.add, A.mult)
-        vz = V([vl], "tt", Z[:, 0:128:16], L[:, 15:128:16], bank[:, 143:256:16], A.add)
-        return vz, vl, V([vz], "scan", G[:, 1:129], Z[:, 0:128], T.msk[:, 128 * p + 128:128 * p + 256], 0.0, A.add, A.mult)
+        vo = V([tok, late["msk"]], "scan", O[:, 0:128], T.msk[:, 272:400], bank[:, 0:128], 0.0, A.mult, A.add)
+        vl = V([], "scan", T.L[:, 128 * p:128 * p + 128], bank[:, 127:255], RT, 0.0, A.mult, A.max)
+        return V([vo], "scan", G[:, 1:129], O[:, 15:143], T.msk[:, 0:128], 0.0, A.max, A.mult), vl
 
-    def places(p):
-        Z, G = ZG[p], ZG[2 + p]
-        return [(T.b4[:, 0:34], Z[:, 0:128], T.Q[:, 0:2, :], False, False),
-                (T.b4[:, 0:34], G[:, 0:128], T.Q[:, 0:2, :], False, False),
-                (T.b4[:, 0:34], G[:, 1:129], T.Q[:, 2:4, :], False, p == 1)]
+    def fields(bank, c0):
+        jobs = tlist(bank, T.R2, c0, B2, 24, False, True)
+        src = jobs[15][1]
+        return jobs[:15] + [(bank[:, 14:128:16], src, B2[:, 0:8], False, False), (bank[:, 143:384:16], src, B2[:, 8:24], False, True)]
 
-    def before(p):
-        return [(T.b2[:, 0:256], T.L[:, 128 * p:128 * p + 128], T.PM[:, 256 * p:256 * p + 256], False, p == 1)]
+    def places(p, bank):
+        return [(bank[:, 0:18], G[:, 0:128], T.Q[:, 0:18], False, False),
+                (bank[:, 0:18], G[:, 1:129], T.Q[:, 18:36], False, True)]
 
-    MM([c_late, v_jl[2], d_q], [(T.b4[:, 0:34], ID, CH, True, False), (T.b4[:, 17:34], ID, T.lo[:], False, False),
-                                (T.b2[:, 0:272], moved(E, 0), T.cv[:], True, False)], False)
-    g2.append(V([r_x[3]], "cp", *gx(192, 224)))
-    g2.append(ACT([r_x[3]], *gx(224, 256), F.Copy))
-    v_c0, _, v_g0 = counts(0, T.b0, t_k0)
-    t_k1 = MM(g2 + [v_jl[1]], tlist(T.b1, T.R2, 128, 256, 16))
-    a_k0 = ACT([v_c0], T.kX[:, 0:128], T.b0[:, 0:128], F.Copy)
-    MM([v_g0], before(0) + places(0), False)
+    def choose(bank, tok):
+        return V([tok], "scan", T.p1[:], T.msk[:, 128:272:8], bank[:, 0:18], 0.0, A.mult, A.max)
+
+    def mark(p, v, toks):
+        v = V([v], "cp", T.zl[:, 10 * p:10 * p + 9], T.p1[:, 1:18:2])
+        return V([v] + toks, "cp", T.mk[:].indirect(T.zl[:, 10 * p:10 * p + 9]), T.DT[:, 144 * p:144 * p + 144])
+
+    def before(p, bank):
+        return [(bank[:, 0:144], T.L[:, 128 * p:128 * p + 128], T.PM[:], False, True)]
+
+    def plus(p, bank, kt, first):
+        return [(bank[:, 0:128], kt[:, 128 * p:128 * p + 128], ID, first, not first)]
+
+    def sums(p, bank, tok):
+        return ACT([tok], T.YW[:, 128 * p:128 * p + 128], bank[:, 0:128], F.Identity, 253.0)
+
+    row = [upto[256], p_y]
+    g1 = [ga(0, row), gv(0, row)]
+    jl(3)
+    g1 += [ga(1), gv(1)]
+    t_kf = MM([a_f0], tlist(T.b6[:, 128:256], T.R, 128, B2[:, 16:24], 8, True, True))
+    g2 = [gv(2), ga(2)]
+    a_kf = ACT([t_kf], T.kfs[:, 128:256], T.b6[:, 128:256], F.Copy)
+    r_f = SEND([a_kf], nxc, T.kfl[:], T.kfs[:], "rf")
+    t_k0 = MM(g1 + [late["msk"]], fields(T.b0, 0))
+    MM([v_jl[3], m_mk], columns(1, T.b3), False)
+    v_c0, v_l0 = counts(0, T.b0, t_k0)
+    g2 += [gv(3), ga(3)]
+    t_l0 = MM([v_l0], before(0, T.b5))
+    t_z0 = MM([v_c0, late["q"]], places(0, T.b4))
+    t_k1 = MM(g2, fields(T.b1, 128))
+    a_dt0 = ACT([t_l0], T.DT[:, 0:144], T.b5[:, 0:144], F.Copy)
+    a_k0 = ACT([v_l0], T.kX[:, 0:128], T.b0[:, 256:384], F.Identity, -256.0)
+    v = choose(T.b4, t_z0)
+    v_all = V([], "scan", T.H[:], T.msk[:, 128:256], O[:, 15:143], 0.0, A.mult, A.max)
+    v_mk0 = mark(0, v, [a_dt0, d_m])
+    v_c1, v_l1 = counts(1, T.b1, t_k1)
     v_owf = V([l_own], "cp", T.owf[:], T.owi[:])
+    MM([v_all], [(T.b7[:, 0:18], T.H[:], T.Q[:, c:c + 18], False, False) for c in (0, 18)], False)
+    t_y0 = MM([r_f, a_k0], plus(0, T.b4, T.kX, True) + plus(0, T.b4, T.kfl, False))
+    t_l1 = MM([v_l1], before(1, T.b3))
+    t_z1 = MM([v_c1], places(1, T.b7))
     DMA("s", "dwin", [v_owf], T.WB[0::16, 0:4096], T.owf[:])
-    ACT([], T.mk[:, 0:1024], T.R[:, 0:1024], F.Copy, None, 0.0)
-    v_c1, v_l1, v_g1 = counts(1, T.b1, t_k1)
-    a_k1 = ACT([v_c1], T.kX[:, 128:256], T.b1[:, 0:128], F.Copy)
-    t_l1 = MM([v_l1], before(1))
-    t_z = MM([v_g1], places(1))
-    t_y0 = MM([r_f, a_k0], plus(T.b7, T.kX[:, 0:128], False) + plus(T.b7, T.kfl[:, 0:128], True))
-    t_y1 = MM([a_k1], plus(T.b5, T.kfl[:, 128:256], False) + plus(T.b5, T.kX[:, 128:256], True))
-    a_dt = ACT([t_l1], T.DT[:], T.b2[:, 0:272], F.Copy)
-    ACT([t_y0], T.YW[:, 0:128], T.b7[:, 0:128], F.Identity, -3.0)
-    a_yw = ACT([t_y1], T.YW[:, 128:256], T.b5[:, 0:128], F.Identity, -3.0)
-    MM([c_c2], [(T.b0[:, 0:64], ID, T.c2[:], True, False), (T.b0[:, 0:64], ID, T.c2[:], False, False)], False)
-    d_win = DMA("s", "dwin", [a_yw], T.WB[1::16, 0:4096], T.YW[:])
-    v_e1 = V([t_z, d_k], "ts", T.e1[:, 0:16], T.b4[:, 17:33], 0.0, None, A.max)
-    v_p1 = V([v_e1], "tt", T.p1[:], T.e1[:], T.b4[:, 0:17], A.add)
-    v_zl = V([v_p1], "cp", T.zl[:, 0:17], T.p1[:])
-    v_mks = V([v_zl, a_dt], "cp", T.mk[:].indirect(T.zl[:, 0:17]), T.DT[:])
-    v_s0 = V([v_mks, a_d0], "scan", T.S[:, 0:512], T.d0[:], T.mk[:, 0:512], 0.0, A.add, A.max)
-    v_s1 = V([v_s0], "scan", T.S[:, 512:1024], T.d0[:], T.mk[:, 512:1024], T.S[:, 511:512], A.add, A.max)
-    a_h = ACT([v_s0], T.hit[:, 0:512], T.S[:, 0:512], F.Relu, T.K[:, 3:4], T.K[:, 1:2])
-    v_h = V([v_s1], "ts", T.hit[:, 512:1024], T.S[:, 512:1024], 4096.0, T.K[:, 1:2], A.min, A.mult)
-    t_h = MM([a_h, v_h], [(T.b0[:, 0:64], moved(E, t), T.hit[:, t:1024:16], False, t == 15) for t in range(16)])
-    v_o = V([t_h], "ts", T.off[:], T.b0[:, 0:64], 0.0625, None, A.mult)
+    a_k1 = ACT([v_l1], T.kX[:, 128:256], T.b1[:, 256:384], F.Identity, -256.0)
+    a_dt1 = ACT([t_l1], T.DT[:, 144:288], T.b3[:, 0:144], F.Copy)
+    sums(0, T.b4, t_y0)
+    t_y1 = MM([a_k1], plus(1, T.b0, T.kfl, True) + plus(1, T.b0, T.kX, False))
+    d_win = DMA("s", "dwin", [sums(1, T.b0, t_y1)], T.WB[1::16, 0:4096], T.YW[:])
+    v_mk1 = mark(1, choose(T.b7, t_z1), [a_dt1, v_mk0])
+    v_s = V([v_mk1, d_g], "scan", T.S[:], T.d0[:], T.mk[:, 0:1024], CAP, A.mult, A.min)
+    t_h = MM([v_s], rewrap(T.b2[:, 0:64], E, T.S, 0, 64))
+    v_o = V([t_h], "ts", T.off[:], T.b2[:, 0:64], 256.0 / CAP, None, A.mult)
     win = T.WB[:, 0:4112]
     a_r = ACT([v_o, d_win], T.res[:, 0:512], win.indirect(T.off[:, 0:32]), F.Copy)
     v_r = V([v_o, d_win], "cp", T.res[:, 512:1024], win.indirect(T.off[:, 32:64]))

from concourse.mybir import AluOpType as A, ActivationFunctionType as F

SCRATCH = {
    "owi": ("sbuf", [128, 256], "int32"),
    "pti": ("sbuf", [128, 256], "int32"),
    "nxi": ("sbuf", [128, 256], "int32"),
    "ols": ("sbuf", [128, 256], "uint16"),
    "ol": ("sbuf", [128, 256], "uint16"),
    "pfs": ("sbuf", [128, 256], "float32"),
    "pf": ("sbuf", [128, 256], "float32"),
    "pb": ("sbuf", [128, 256], "bfloat16"),
    "nls": ("sbuf", [128, 256], "uint16"),
    "nl": ("sbuf", [128, 256], "uint16"),
    "jl": ("sbuf", [128, 256], "uint16"),
    "jx": ("sbuf", [128, 256], "uint16"),
    "D": ("sbuf", [128, 2048], "float32"),
    "WA": ("sbuf", [128, 8192], "bfloat16"),
    "WB": ("sbuf", [128, 8192], "float32"),
    "bg": ("sbuf", [128, 4096], "bfloat16"),
    "R": ("sbuf", [128, 4112], "bfloat16"),
    "R2": ("sbuf", [128, 4096], "bfloat16"),
    "prow": ("sbuf", [8, 4096], "bfloat16"),
    "pid": ("sbuf", [128, 1], "int32"),
    "h8": ("sbuf", [128, 1], "int32"),
    "o1": ("sbuf", [128, 1], "int32"),
    "s16": ("sbuf", [128, 1], "float32"),
    "sc": ("sbuf", [128, 1], "float32"),
    "ev": ("sbuf", [128, 1], "float32"),
    "u4": ("sbuf", [128, 1], "float32"),
    "jj": ("sbuf", [128, 8], "float32"),
    "hb": ("sbuf", [128, 8], "float32"),
    "xx": ("sbuf", [128, 256], "float32"),
    "K": ("sbuf", [128, 1], "float32"),
    "K2": ("sbuf", [128, 4], "float32"),
    "BZ": ("sbuf", [128, 1208], "bfloat16"),
    "Q": ("sbuf", [128, 80], "bfloat16"),
    "lo": ("sbuf", [128, 18], "bfloat16"),
    "one": ("sbuf", [128, 144], "bfloat16"),
    "msk": ("sbuf", [128, 400], "bfloat16"),
    "PM": ("sbuf", [128, 144], "bfloat16"),
    "H": ("sbuf", [128, 128], "bfloat16"),
    "L": ("sbuf", [128, 256], "bfloat16"),
    "cv": ("sbuf", [33, 144], "bfloat16"),
    "d0": ("sbuf", [128, 1024], "bfloat16"),
    "mk": ("sbuf", [128, 7520], "bfloat16"),
    "S": ("sbuf", [128, 1024], "bfloat16"),
    "off": ("sbuf", [128, 64], "uint16"),
    "kX": ("sbuf", [128, 256], "bfloat16"),
    "kfs": ("sbuf", [128, 256], "bfloat16"),
    "kfl": ("sbuf", [128, 256], "bfloat16"),
    "DT": ("sbuf", [128, 288], "bfloat16"),
    "p1": ("sbuf", [128, 18], "float32"),
    "zl": ("sbuf", [128, 20], "uint16"),
    "YW": ("sbuf", [128, 256], "float32"),
    "owf": ("sbuf", [128, 256], "float32"),
    "res": ("sbuf", [128, 1024], "float32"),
}
for _k in range(8):
    SCRATCH["b%d" % _k] = ("psum", [128, 512], "float32")
SEMAPHORES = ["v", "a", "t", "p", "down", "dpts", "dnxt", "dd", "dz", "dprow", "dk", "dq", "dw", "dy", "dm", "dg", "dwin", "dout",
              "rp", "ro", "rn", "rx0", "rx1", "rx2", "rx3", "rf", "sent"]

SUBS = [(k, k + 32) for k in range(0, 256, 32)]
XZ, XA, XD, XV, XP1 = 896, 4384, 5920, 6360, 512
W0, PRE = 576, 0
NV = 5
G2 = (38, 24, 48, 10)
GROW, CAP = 2.0 ** 14, 2.0 ** 99


def rank_program(g, core, T, topo):
    rank = T.rank_of(core)
    if rank is None:
        return
    prv, nxc, opp = (T.cores[(rank + k) % 4] for k in (3, 1, 2))
    queues = {"v": g.vector, "a": g.scalar, "t": g.tensor, "p": g, "s": g.sync}
    cnt = {}
    seen = {}

    def need(q, toks):
        best = {}
        for s, n in toks:
            best[s] = max(best.get(s, 0), n)
        for s in sorted(best):
            if seen.get((q, s), 0) < best[s]:
                queues[q].wait_ge(T.sem[s], best[s])
                seen[(q, s)] = best[s]

    def done(s, ins, n):
        cnt[s] = cnt.get(s, 0) + n
        ins.then_inc(T.sem[s], n)
        return (s, cnt[s])

    def V(toks, name, *args):
        need("v", toks)
        q = g.vector
        if name == "ts":
            out, in0, s1, s2, op0 = args[:5]
            ins = q.tensor_scalar(out, in0, s1, s2, op0, args[5]) if len(args) > 5 else q.tensor_scalar(out, in0, s1, s2, op0)
        elif name == "tt":
            ins = q.tensor_tensor(*args)
        elif name == "cp":
            ins = q.tensor_copy(*args)
        elif name == "ms":
            ins = q.memset(*args)
        else:
            ins = q.tensor_tensor_scan(*args)
        return done("v", ins, 1)

    def ACT(toks, out, in_, func, bias=None, scale=None):
        need("a", toks)
        if scale is not None and bias is not None:
            ins = g.scalar.activation(out, in_, func, bias=bias, scale=scale)
        elif scale is not None:
            ins = g.scalar.activation(out, in_, func, scale=scale)
        elif bias is not None:
            ins = g.scalar.activation(out, in_, func, bias=bias)
        else:
            ins = g.scalar.activation(out, in_, func)
        return done("a", ins, 1)

    def IOTA(toks, out, pattern, base, cm, small=True):
        need("p", toks)
        ins = g.iota(out, pattern, base, cm, allow_small_or_imprecise_dtypes=True) if small else g.iota(out, pattern, base, cm)
        return done("p", ins, 1)

    def SEL(toks, buf, pattern, cmp, fill, base, cm, src=None):
        need("p", toks)
        return done("p", g.affine_select(buf, buf if src is None else src, pattern, cmp, fill, base, cm), 1)

    def DMA(q, s, toks, out, in_):
        need(q, toks)
        return done(s, queues[q].dma_start(out, in_), 16)

    def MM(toks, jobs, tok=True):
        need("t", toks)
        ins = None
        for out, lhs, rhs, st, sp in jobs:
            ins = g.tensor.matmul(out, lhs, rhs, st, sp)
        return done("t", ins, 1) if tok else None

    def SEND(toks, to, dst, src, sem, part=slice(None)):
        need("p", toks)
        rid, pid, _se = topo.addr(to)
        engines = topo.engines(core, to)[part]
        g.remote_dma(out_ap=dst, in_ap=src, remote_sem=T.sem[sem], local_sem=T.sem.sent, pid=pid, routing_id=rid,
                     dma_engine_mask=sum(1 << e for e in engines))
        n = len(engines)
        cnt["sent"] = cnt.get("sent", 0) + n
        cnt[sem] = cnt.get(sem, 0) + n
        return (sem, cnt[sem])

    def moved(mat, t, K=128):
        buf, c = mat
        return buf[0:K, c + 15 - t:c + 143 - t]

    def rewrap(out, mat, src, c0, c1, K=128, alone=True):
        return [(out, moved(mat, t, K), src[0:K, 16 * c0 + t:16 * c1:16], alone and t == 0, alone and t == 15) for t in range(16)]

    def el(buf, c0, c1):
        return buf[:, 16 * c0:16 * c1]

    l_own = DMA("s", "down", [], T.owi[:], T.own[:])
    l_pts = DMA("s", "dpts", [], T.pti[:], T.pts[:])

    c_pid = IOTA([], T.pid[:], [[1, 1]], 0, 1, False)
    c_j = IOTA([], T.jj[:], [[-4, 8]], 48, 0)
    c_x = IOTA([], T.xx[:], [[1, 256]], 0, 0)
    z0 = V([], "ms", T.WB[:, 0:64], 0.0)
    z1 = V([], "ms", T.WB[:, 128:XZ], 0.0)
    v_h8 = V([c_pid], "ts", T.h8[:], T.pid[:], 8, None, A.bitwise_and)
    v_o1 = V([], "ts", T.o1[:], T.pid[:], 5, None, A.bitwise_and)
    v_s = V([v_h8], "ts", T.s16[:], T.h8[:], 4.0, -16.0, A.mult, A.add)
    v_sc = V([v_s, v_o1], "ts", T.sc[:], T.o1[:], 1.0, T.s16[:], A.is_equal, A.mult)
    V([], "ts", T.u4[:], T.o1[:], -127.0, T.s16[:], A.mult, A.add)
    v_ev = V([v_sc], "ts", T.ev[:], T.s16[:], T.sc[:], None, A.subtract)
    V([], "ms", T.WA[:, 0:W0], 0.0)
    v_ols = V([l_own], "cp", T.ols[:], T.owi[:])
    v_bias = V([v_ev, c_j], "ts", T.hb[:], T.jj[:], T.u4[:], T.ev[:], A.subtract, A.mult)
    v_wa0 = V([], "ms", T.WA[:, W0:1024], 0.0)
    v_pf = V([l_pts], "ts", T.pfs[:], T.pti[:], 1.0, T.s16[:], A.add, A.mult)
    a1 = ACT([z0], T.WB[:, 64:128], T.WB[:, 0:64], F.Silu)
    a5 = ACT([a1, z1], T.WB[:, XZ:2 * XZ], T.WB[:, 0:XZ], F.Silu)
    for j in range(8):
        out = T.D[:, 256 * j:256 * j + 256]
        if j < NV:
            v_d = V([v_bias, c_x], "ts", out, T.xx[:], T.sc[:], T.hb[:, j:j + 1], A.mult, A.add)
        else:
            a_d = ACT([v_bias, c_x], out, T.xx[:], F.Identity, T.hb[:, j:j + 1], T.sc[:])
    for c in range(2 * XZ, XA, 2 * XZ):
        a_wb = ACT([a5], T.WB[:, c:min(c + 2 * XZ, XA)], T.WB[:, 0:min(2 * XZ, XA - c)], F.Silu)
    v_wb = V([], "ms", T.WB[:, XD:XV], 0.0)
    v_wa = V([], "ms", T.WA[:, 2048:8192], 0.0)

    def clear(c0, c1):
        return IOTA([], T.WB[:, c0:c1], [[0, c1 - c0]], 0, 0)

    clear(XV, XV + XP1)
    r_o = SEND([v_ols], opp, T.ol[:], T.ols[:], "ro", slice(1, None, 4))
    r_p = SEND([v_pf], opp, T.pf[:], T.pfs[:], "rp", slice(0, None, 2))
    p_z2 = clear(XV + XP1, 8192)

    for c in range(XA, XD, XZ - 128):
        DMA("s", "dd", [z1], T.WB[:, c:c + XZ - 128], T.WB[:, 128:XZ])
    DMA("s", "dz", [v_wa0], T.WA[:, 1024:2048], T.WA[:, 0:1024])
    d_d = DMA("s", "dd", [r_p, a_d, v_d], T.D[2::8, :], T.pf[:])
    l_nxt = DMA("s", "dnxt", [], T.nxi[:], T.nxt[:])
    p_z = DMA("s", "dz", [v_wa0], T.BZ[:, 0:496], T.WA[:, 0:496])
    v_nls = V([l_nxt], "cp", T.nls[:], T.nxi[:])

    s_b = ACT([a_wb, v_wb, p_z2, r_o, d_d], T.WB[:].indirect(T.ol[:, 128:256]), T.D[:], F.Silu)
    s_a = V([v_wa, r_o, d_d, p_z], "cp", T.WA[:].indirect(T.ol[:, 0:128]), T.D[:])

    BY, CH, G, O = T.BZ[0:8, 0:16], T.BZ[:, 16:34], T.BZ[:, 39:168], T.BZ[:, 168:311]
    BI, E = (T.BZ, 296), (T.BZ, 424)
    B2 = T.BZ[:, 567:936:16]
    ALL = T.BZ[:, 311:936:16]
    RT = T.BZ[:, 952:1080]
    ID = T.BZ[:, 1080:1208]
    NIL, ONE = T.BZ[0:1, 40:168], T.one[0:1, 0:128]
    DMA("s", "dy", [p_z], T.BZ[:, 496:952], T.BZ[:, 40:496])
    p_y = DMA("s", "dy", [], T.R[:, 4096:4112], T.BZ[:, 40:56])

    def repeat(sem, tok, cols, k):
        for n in (k, 4 * k):
            for b in (n, 2 * n, 3 * n):
                e = min(b + n, 128)
                d = DMA("s", sem, [tok], T.Q[b:e, cols], T.Q[0:e - b, cols])
            tok = d
        return tok

    m_pb = SEL([v_pf], T.pb[:], [[0, 256]], A.is_equal, 0.0, 0, 0, T.pfs[:])
    m = IOTA([], T.Q[0:9, :], [[0, 80]], 0, 0)
    IOTA([], T.K[:], [[0, 1]], int(GROW), 0)
    IOTA([m], T.Q[0:8, 48:56], [[0, 8]], 1, 0)
    m0 = SEL([], T.Q[0:8, 40:48], [[0, 8]], A.not_equal, 4.0, 0, 1)
    m1 = SEL([], T.Q[0:8, 56:72], [[0, 16]], A.not_equal, -129.0 / 2 ** 20, 0, 1)
    SEL([], T.Q[0:8, 72:80], [[0, 8]], A.not_equal, -0.0625, -2, 1)
    SEL([m0], T.Q[0:8, 40:48], [[0, 8]], A.not_equal, -0.0625, -1, 1)
    m_w = SEL([m1], T.Q[0:8, 56:72], [[0, 16]], A.not_equal, 129.0 / 2 ** 20, -4, 1)
    r_n = SEND([v_nls], prv, T.nl[:], T.nls[:], "rn")
    d_prow = DMA("s", "dprow", [m_pb], T.prow[:], T.pb[:])
    d_w = repeat("dw", m_w, slice(40, 80), 8)
    SEL([p_z], BY[:, 0:8], [[-1, 8]], A.not_equal, -0.0625, 0, 1)
    m_by = SEL([], BY[:, 8:16], [[-1, 8]], A.not_equal, 0.0625, 0, 1)
    c_k = IOTA([], T.K2[:], [[-1, 2], [1, 2]], 0, 0)
    p_one = IOTA([], T.one[:], [[0, 144]], 1, 0)
    m_mk = SEL([p_one], T.mk[:, 0:128], [[0, 128]], A.not_equal, CAP, 0, 0, T.one[:, 0:128])
    SEL([p_y], ID, [[-1, 128]], A.is_equal, 0.0, 0, 1, T.one[:, 0:128])
    SEL([m_mk], RT, [[0, 8], [1, 16]], A.is_equal, 0.0, 0, 0, T.mk[:, 0:128])
    m = SEL([d_w], ALL, [[0, 5], [-16, 8]], A.is_ge, 0.0, 0, 1, T.Q[:, 40:80])
    IOTA([], CH[:, 1:18:2], [[0, 9]], 6144, -32)
    m_bi = SEL([m], ALL, [[0, 5], [16, 8]], A.is_ge, 0.0, 15, -1)
    IOTA([], T.lo[:], [[432, 2], [-2, 9]], 0, 0)
    SEL([m_bi], ALL[:, 8:16], [[-16, 8]], A.not_equal, -1.0 / 256, 0, 1)
    c_cv = IOTA([], T.cv[:], [[-1, 9], [9, 16]], -136, -4)

    def tlist(out, src, c0, mat, n, start, stop, K=128):
        return [(out[:, t:16 * n:16], src[0:K, 16 * c0 + t:16 * c0 + 2048:16], mat, start, start or (stop and t == 15))
                for t in range(16)]

    for p, bank in enumerate((T.b0, T.b1)):
        MM([m_by, d_prow], [(bank[:, 0:384], NIL, T.prow[0:1, 0:384], True, False)]
           + tlist(bank[:, 256:384], T.prow, 128 * p, BY[:, 8 * p:8 * p + 8], 8, False, False, 8), False)
    MM([p_one], [(bank[:, 128:256], ONE, ONE, False, False) for bank in (T.b0, T.b1)], False)

    d_k = DMA("s", "dk", [c_k], T.K[0::16, :], T.K2[0:8, 1:2])
    d_m = m_mk
    for b in (128, 256, 512):
        d_m = DMA("s", "dm", [d_m], T.mk[:, b:2 * b], T.mk[:, 0:b])

    def columns(p, bank):
        jobs = [(bank[:, 0:144], RT[32 * p:32 * p + 1, :], T.cv[32 * p:32 * p + 1, :], True, False)]
        return jobs + [(bank[:, 0:1], lhs[32:33, 0:128], T.one[32:33, 0:1], False, False) for lhs in (T.mk, RT)] * p

    def spare(p, bank):
        return [(bank[:, 0:18], ID, CH, True, False), (bank[:, 1:18:2], ID, T.lo[:, 0:9], False, False),
                (bank[:, 2 * p:18:2], moved(E, 0), T.lo[:, 9 + p:18], False, False),
                (bank[:, 1:18:2], RT[0:1, :], T.cv[0:1, 0:9], False, False)]

    g_a = [ACT([s_b, r_n], el(T.bg, c0, c1), T.WB[:].indirect(T.nl[:, c0:c1]), F.Copy, None, -1.0) for c0, c1 in SUBS]
    upto = {}
    t_code = [None] * 4
    v_jl = [None] * 4
    r_x = [None] * 4
    code = [T["b%d" % (2 + q % 2)][:, 0:64] for q in range(4)]
    late = {}

    def jl(q):
        cols = slice(64 * q, 64 * q + 64)
        v_jl[q] = V([t_code[q]], "ts", T.jl[:, cols], code[q], 4096.0, None, A.add)
        r_x[q] = SEND([v_jl[q]], nxc, T.jx[:, cols], T.jl[:, cols], "rx%d" % q)
        if q == 0:
            SEL([], T.Q[0:9, 0:18:2], [[-1, 9]], A.is_ge, 1.0, 0, 1)
            SEL([], T.Q[0:9, 1:18:2], [[-1, 9]], A.not_equal, -8192.0, 0, 1)
            SEL([], T.Q[0:9, 18:36:2], [[1, 9]], A.is_gt, 1.0, 0, -1)
            m_q = SEL([], T.Q[0:9, 19:36:2], [[-1, 9]], A.not_equal, 8192.0, 0, 1)
            late["q"] = repeat("dq", m_q, slice(0, 40), 9)
            SEL([], T.msk[:, 0:128], [[0, 8], [-9, 16]], A.is_ge, 0.0, 134, -1, T.one[:, 0:128])
        if q == 1:
            m = SEL([], T.msk[:, 128:272], [[0, 9], [1, 16]], A.not_equal, 0.0, 0, 0, T.one[:])
            SEL([], T.PM[:], [[-1, 9], [9, 16]], A.is_equal, 0.0, -135, 1, T.one[:])
            late["msk"] = SEL([m], T.msk[:, 272:400], [[0, 8], [1, 16]], A.not_equal, -1.0, -15, 0, T.msk[:, 128:256])

    for k, (c0, c1) in enumerate(SUBS):
        upto[c1] = V([s_a, g_a[k], r_n], "tt", el(T.R, c0, c1), T.WA[:].indirect(T.nl[:, c0:c1]), el(T.bg, c0, c1), A.min)
        if c1 % 64 == 0:
            q = c1 // 64 - 1
            t_code[q] = MM([upto[c1], m_bi] + ([v_jl[q - 2]] if q > 1 else []), rewrap(code[q], BI, T.R, 64 * q, 64 * q + 64))
            if q == 1:
                t_p0 = MM([], tlist(T.b6[:, 0:128], T.R, 0, B2[:, 16:24], 8, True, True))
            if q == PRE:
                MM([c_cv], spare(0, T.b4) + columns(0, T.b5) + spare(1, T.b7), False)
        if c1 in (128, 192, 256):
            jl(c1 // 64 - 2)
    a_f0 = ACT([t_p0], T.kfs[:, 0:128], T.b6[:, 0:128], F.Copy)
    a_d0 = ACT([d_k, g_a[0]], T.d0[:, 0:512], T.bg[:, 0:512], F.Identity, T.K[:, 0:1], 0.0)
    DMA("s", "dwin", [d_k, g_a[-1]], T.WB[0::16, 4102:4103], T.K2[0:8, 2:3])
    DMA("s", "dwin", [], T.WB[1::16, 4102:4103], T.K2[0:8, 0:1])
    d_g = DMA("s", "dg", [a_d0], T.d0[:, 512:1024], T.d0[:, 0:512])

    def gv(q, toks=()):
        c0, c1 = 64 * q, 64 * q + G2[q]
        return V(list(toks) + [r_x[q]], "cp", el(T.R2, c0, c1), T.R[:].indirect(T.jx[:, c0:c1]))

    def ga(q, toks=()):
        c0, c1 = 64 * q + G2[q], 64 * q + 64
        return ACT(list(toks) + [r_x[q]], el(T.R2, c0, c1), T.R[:].indirect(T.jx[:, c0:c1]), F.Copy)

    def counts(p, bank, tok):
        vo = V([tok, late["msk"]], "scan", O[:, 0:128], T.msk[:, 272:400], bank[:, 0:128], 0.0, A.mult, A.add)
        vl = V([], "scan", T.L[:, 128 * p:128 * p + 128], bank[:, 127:255], RT, 0.0, A.mult, A.max)
        return V([vo], "scan", G[:, 1:129], O[:, 15:143], T.msk[:, 0:128], 0.0, A.max, A.mult), vl

    def fields(bank, c0):
        jobs = tlist(bank, T.R2, c0, B2, 24, False, True)
        src = jobs[15][1]
        return jobs[:15] + [(bank[:, 14:128:16], src, B2[:, 0:8], False, False), (bank[:, 143:384:16], src, B2[:, 8:24], False, True)]

    def places(p, bank):
        return [(bank[:, 0:18], G[:, 0:128], T.Q[:, 0:18], False, False),
                (bank[:, 0:18], G[:, 1:129], T.Q[:, 18:36], False, True)]

    def choose(bank, tok):
        return V([tok], "scan", T.p1[:], T.msk[:, 128:272:8], bank[:, 0:18], 0.0, A.mult, A.max)

    def mark(p, v, toks):
        v = V([v], "cp", T.zl[:, 10 * p:10 * p + 9], T.p1[:, 1:18:2])
        return V([v] + toks, "cp", T.mk[:].indirect(T.zl[:, 10 * p:10 * p + 9]), T.DT[:, 144 * p:144 * p + 144])

    def before(p, bank):
        return [(bank[:, 0:144], T.L[:, 128 * p:128 * p + 128], T.PM[:], False, True)]

    def plus(p, bank, kt, first):
        return [(bank[:, 0:128], kt[:, 128 * p:128 * p + 128], ID, first, not first)]

    def sums(p, bank, tok):
        return ACT([tok], T.YW[:, 128 * p:128 * p + 128], bank[:, 0:128], F.Identity, 253.0)

    row = [upto[256], p_y]
    g1 = [ga(0, row), gv(0, row)]
    jl(3)
    g1 += [ga(1), gv(1)]
    t_kf = MM([a_f0], tlist(T.b6[:, 128:256], T.R, 128, B2[:, 16:24], 8, True, True))
    g2 = [gv(2), ga(2)]
    a_kf = ACT([t_kf], T.kfs[:, 128:256], T.b6[:, 128:256], F.Copy)
    r_f = SEND([a_kf], nxc, T.kfl[:], T.kfs[:], "rf")
    t_k0 = MM(g1 + [late["msk"]], fields(T.b0, 0))
    MM([v_jl[3], m_mk], columns(1, T.b3), False)
    v_c0, v_l0 = counts(0, T.b0, t_k0)
    g2 += [gv(3), ga(3)]
    t_l0 = MM([v_l0], before(0, T.b5))
    t_z0 = MM([v_c0, late["q"]], places(0, T.b4))
    t_k1 = MM(g2, fields(T.b1, 128))
    a_dt0 = ACT([t_l0], T.DT[:, 0:144], T.b5[:, 0:144], F.Copy)
    a_k0 = ACT([v_l0], T.kX[:, 0:128], T.b0[:, 256:384], F.Identity, -256.0)
    v = choose(T.b4, t_z0)
    v_all = V([], "scan", T.H[:], T.msk[:, 128:256], O[:, 15:143], 0.0, A.mult, A.max)
    v_mk0 = mark(0, v, [a_dt0, d_m])
    v_c1, v_l1 = counts(1, T.b1, t_k1)
    v_owf = V([l_own], "cp", T.owf[:], T.owi[:])
    MM([v_all], [(T.b7[:, 0:18], T.H[:], T.Q[:, c:c + 18], False, False) for c in (0, 18)], False)
    t_y0 = MM([r_f, a_k0], plus(0, T.b4, T.kX, True) + plus(0, T.b4, T.kfl, False))
    t_l1 = MM([v_l1], before(1, T.b3))
    t_z1 = MM([v_c1], places(1, T.b7))
    DMA("s", "dwin", [v_owf], T.WB[0::16, 0:4096], T.owf[:])
    a_k1 = ACT([v_l1], T.kX[:, 128:256], T.b1[:, 256:384], F.Identity, -256.0)
    a_dt1 = ACT([t_l1], T.DT[:, 144:288], T.b3[:, 0:144], F.Copy)
    sums(0, T.b4, t_y0)
    t_y1 = MM([a_k1], plus(1, T.b0, T.kfl, True) + plus(1, T.b0, T.kX, False))
    d_win = DMA("s", "dwin", [sums(1, T.b0, t_y1)], T.WB[1::16, 0:4096], T.YW[:])
    v_mk1 = mark(1, choose(T.b7, t_z1), [a_dt1, v_mk0])
    v_s = V([v_mk1, d_g], "scan", T.S[:], T.d0[:], T.mk[:, 0:1024], CAP, A.mult, A.min)
    t_h = MM([v_s], rewrap(T.b2[:, 0:64], E, T.S, 0, 64))
    v_o = V([t_h], "ts", T.off[:], T.b2[:, 0:64], 256.0 / CAP, None, A.mult)
    win = T.WB[:, 0:4112]
    a_r = ACT([v_o, d_win], T.res[:, 0:512], win.indirect(T.off[:, 0:32]), F.Copy)
    v_r = V([v_o, d_win], "cp", T.res[:, 512:1024], win.indirect(T.off[:, 32:64]))
    DMA("s", "dout", [a_r, v_r], T.yk[:], T.res[0::16, :])
    DMA("a", "dout", [a_r, v_r], T.ys[:], T.res[1::16, :])
    need("p", [(s, cnt[s]) for s in sorted(cnt)])
